import numpy as np
import ml_dtypes


def mxq(x, axis, fmt="e4m3"):
    dtype, down = {"e4m3": (ml_dtypes.float8_e4m3fn, 7), "e5m2": (ml_dtypes.float8_e5m2, 14)}[fmt]
    v = np.moveaxis(np.asarray(x, np.float32).astype(ml_dtypes.bfloat16).astype(np.float64), axis, -1)
    blocks = v.reshape(v.shape[:-1] + (-1, 32))
    amax = np.abs(blocks).max(-1, keepdims=True)
    byte = np.maximum(np.where(amax > 0, np.frexp(amax)[1] - 1 + 127, 0) - down, 1)
    scale = np.exp2(byte - 127.0)
    codes = (blocks / scale).astype(np.float32).astype(dtype).astype(np.float64)
    return np.moveaxis((codes * scale).reshape(v.shape), -1, axis)


WIDE = False


def mx_kscale(k):
    if not WIDE:
        return np.ones(k)
    levels = np.array([10, -10, 5, -5, 0])
    if k % 512:
        return np.exp2(np.random.permutation(np.resize(levels, k // 32))).repeat(32)
    a = np.empty((k // 512, 16))
    for p in range(k // 512):
        a[p, :8] = np.random.permutation(np.resize(levels, 8))
        for g in range(8):
            far = levels[np.abs(levels - a[p, g]) >= 10]
            a[p, g + 8] = far[np.random.randint(len(far))]
    return np.exp2(a.ravel()).repeat(32)


BF16 = ml_dtypes.bfloat16


def bf(x):
    return np.asarray(x, np.float32).astype(BF16)


def f64(x):
    return np.asarray(x).astype(np.float64)


E2M1 = np.array([0.0, 0.5, 1.0, 1.5, 2.0, 3.0, 4.0, 6.0, -0.0, -0.5, -1.0, -1.5, -2.0, -3.0, -4.0, -6.0])


def pack_weight(w, fmt):
    k, n = w.shape
    w = f64(bf(w)).reshape(k // 32, 32, n)
    amax = np.abs(w).max(1)
    if fmt == "e4m3":
        byte = np.frexp(amax)[1] - 1 + 127 - 7
    else:
        mant, ex = np.frexp(amax / 6.0)
        byte = np.where(mant > 0.5, ex, ex - 1) + 127
    byte = np.clip(np.where(amax > 0, byte, 1), 1, 254)
    scaled = (w * np.exp2(127.0 - byte)[:, None, :]).reshape(k, n).astype(np.float32)
    by_word = np.ascontiguousarray(scaled.reshape(k // 512, 128, 4, n).transpose(0, 1, 3, 2))
    if fmt == "e4m3":
        words = by_word.astype(ml_dtypes.float8_e4m3fn).view(np.uint8)
    else:
        c = by_word.astype(ml_dtypes.float4_e2m1fn).view(np.uint8) & 0xF
        words = c[..., 0::2] | (c[..., 1::2] << 4)
    return np.ascontiguousarray(words), np.ascontiguousarray(byte.astype(np.uint8).reshape(k // 512, 16, n))


def unpack_weight(words, scales, fmt):
    g, p, n, _ = words.shape
    if fmt == "e4m3":
        vals = np.ascontiguousarray(words).view(ml_dtypes.float8_e4m3fn).astype(np.float64)
    else:
        nib = np.empty((g, p, n, 4), np.uint8)
        nib[..., 0::2] = words & 0xF
        nib[..., 1::2] = words >> 4
        vals = E2M1[nib]
    vals = vals * np.repeat(np.exp2(scales.astype(np.float64) - 127.0), 8, axis=1)[..., None]
    return vals.transpose(0, 1, 3, 2).reshape(g * 512, n)
def pack4(w):
    words, scales = pack_weight(w, "e2m1")
    return words.reshape(words.shape[0], 128, -1), scales


def unpack4(words, scales):
    return unpack_weight(words.reshape(words.shape[0], 128, -1, 2), scales, "e2m1")


P, A, F, Q = 1024, 2048, 1024, 512


def setup_inputs():
    s, t = mx_kscale(A), mx_kscale(F)
    h_words, h_scales = pack4(np.random.standard_normal((A, P)) * s[:, None])
    b_words, b_scales = pack4(np.random.standard_normal((A, F)) / np.sqrt(A) / s[:, None])
    c_words, c_scales = pack4(np.random.standard_normal((F, F)) / np.sqrt(F) / t[:, None])
    l_words, l_scales = pack4(np.random.standard_normal((F, Q)) / np.sqrt(F) / t[:, None])
    return {"h_words": h_words, "h_scales": h_scales,
            "b_words": b_words, "b_scales": b_scales,
            "bench": bf(0.4 * np.random.standard_normal(F)),
            "vol": bf((1 + 0.1 * np.random.standard_normal(F)) * t),
            "c_words": c_words, "c_scales": c_scales,
            "own": bf(np.random.uniform(0.3, 0.9, F)),
            "l_words": l_words, "l_scales": l_scales,
            "spec": bf(np.random.uniform(0.2, 0.8, P))}


def reference(h_words, h_scales, b_words, b_scales, bench, vol, c_words, c_scales, own, l_words, l_scales, spec):
    e = (unpack4(h_words, h_scales).T @ unpack4(b_words, b_scales)) - f64(bench)
    x = np.tanh(e)
    z = mxq(x * f64(vol), 1, "e4m3")
    u = (z @ unpack4(c_words, c_scales)) + f64(own) * x
    y = z @ unpack4(l_words, l_scales)
    sigma = np.sqrt(np.mean(np.square(y), axis=1) + f64(spec))
    return u / sigma[:, None], y / sigma[:, None]

@@ -1,0 +1,352 @@
+from contextlib import ExitStack
+
+import concourse.mybir as mybir
+from concourse.masks import make_identity
+
+ASSETS, PORTFOLIOS, FACTORS, DIRECTIONS = 2048, 1024, 1024, 512
+FLOPS = 2 * PORTFOLIOS * (ASSETS * FACTORS + FACTORS * FACTORS + FACTORS * DIRECTIONS)
+
+F32 = mybir.dt.float32
+BF16 = mybir.dt.bfloat16
+I32 = mybir.dt.int32
+U32 = mybir.dt.uint32
+U8 = mybir.dt.uint8
+FP8X4 = mybir.dt.float8_e4m3fn_x4
+FP4X4 = mybir.dt.float4_e2m1fn_x4
+ACT = mybir.ActivationFunctionType
+ALU = mybir.AluOpType
+
+P = 128
+KG = ASSETS // 512
+FG = FACTORS // 512
+NH = 512
+HALVES = PORTFOLIOS // NH
+TILES = PORTFOLIOS // P
+
+
+def tile_stressed_factor_response_f2_kernel(
+    tc, h_words, h_scales, b_words, b_scales, bench, vol, c_words, c_scales, own, l_words, l_scales, spec, out_0, out_1
+):
+    nc = tc.nc
+    with ExitStack() as ctx:
+        keep = ctx.enter_context(tc.tile_pool(name="keep", bufs=1))
+        work = ctx.enter_context(tc.tile_pool(name="work", bufs=4))
+        psum = ctx.enter_context(tc.psum_pool(name="psum", bufs=8))
+        ctx.enter_context(tc.manual_schedule())
+
+        bw_raw = keep.tile([P, KG, 2 * FACTORS], U8, name="bw_raw", align_bytes=64)
+        bs_raw = keep.tile([P, KG, FACTORS], U8, name="bs_raw", align_bytes=64)
+        bw = keep.tile([P, KG, 2 * FACTORS], U8, name="bw", align_bytes=64)
+        bs = keep.tile([P, KG, FACTORS], U8, name="bs", align_bytes=64)
+        hw = keep.tile([P, KG, 2 * PORTFOLIOS], U8, name="hw", align_bytes=64)
+        hs = keep.tile([P, KG, PORTFOLIOS], U8, name="hs", align_bytes=64)
+        cw = keep.tile([P, FG, 2 * FACTORS], U8, name="cw", align_bytes=64)
+        cs = keep.tile([P, FG, FACTORS], U8, name="cs", align_bytes=64)
+        lw = keep.tile([P, FG, 2 * DIRECTIONS], U8, name="lw", align_bytes=64)
+        ls = keep.tile([P, FG, DIRECTIONS], U8, name="ls", align_bytes=64)
+        bench_b = keep.tile([P, FG, 4], BF16, name="bench_b")
+        vol_b = keep.tile([P, FG, 4], BF16, name="vol_b")
+        own_b = keep.tile([P, FG, 4], BF16, name="own_b")
+        neg_bench = keep.tile([P, FG * 4], F32, name="neg_bench")
+        own_f = keep.tile([P, FG * 4], F32, name="own_f")
+        spec_rows = keep.tile([P, P], BF16, name="spec_rows")
+        spec_f = keep.tile([P, TILES], F32, name="spec_f")
+        ident_b = keep.tile([P, P], BF16, name="ident_b")
+        ident = keep.tile([P, P], F32, name="ident")
+        minus_half = keep.tile([P, 1], F32, name="minus_half")
+        ms = keep.tile([P, TILES], F32, name="ms")
+        var = keep.tile([P, TILES], F32, name="var")
+        rs = keep.tile([P, TILES], F32, name="rs")
+        warm = keep.tile([P, 1], F32, name="warm")
+        idle = keep.tile([P, 512], BF16, name="idle")
+
+        def flat_i32(t):
+            return t[:].rearrange("p g n -> p (g n)").bitcast(I32)
+
+        def load_scales(queue, plane, src):
+            for q in range(4):
+                queue.dma_start(
+                    out=plane[32 * q : 32 * q + 4, :, :].bitcast(I32),
+                    in_=src[:, 4 * q : 4 * q + 4, :].rearrange("g r n -> r g n").bitcast(I32),
+                )
+
+        def by_factor(v):
+            return v.rearrange("(g p t) -> p g t", g=FG, t=4)
+
+        nc.vector.memset(flat_i32(bs_raw), 0)
+        nc.vector.memset(warm[:], 0.0)
+        nc.gpsimd.memset(idle[:], 0.0)
+        nc.gpsimd.memset(flat_i32(hs), 0)
+        nc.gpsimd.memset(spec_rows[:], 0.0)
+        nc.gpsimd.memset(flat_i32(cs), 0)
+        nc.gpsimd.memset(flat_i32(ls), 0)
+        nc.gpsimd.memset(minus_half[:], -0.5)
+        make_identity(nc, ident[:])
+        make_identity(nc, ident_b[:])
+
+        def load_b(g):
+            nc.sync.dma_start(out=bw_raw[:, g, :].bitcast(I32), in_=b_words[g].bitcast(I32))
+
+        def load_h(g, h):
+            cols = slice(2 * NH * h, 2 * NH * (h + 1))
+            nc.sync.dma_start(out=hw[:, g, cols].bitcast(I32), in_=h_words[g][:, cols].bitcast(I32))
+
+        load_b(0)
+        load_h(0, 0)
+        load_scales(nc.sync, bs_raw, b_scales)
+        load_scales(nc.sync, hs, h_scales)
+        nc.scalar.activation(out=warm[:], in_=warm[:], func=ACT.Tanh)
+        for g in range(1, KG):
+            load_b(g)
+            load_h(g, 0)
+        nc.gpsimd.dma_start(out=bench_b[:], in_=by_factor(bench))
+        nc.gpsimd.dma_start(out=vol_b[:], in_=by_factor(vol))
+        nc.gpsimd.dma_start(out=own_b[:], in_=by_factor(own))
+        nc.gpsimd.dma_start(out=spec_rows[0:TILES, :], in_=spec.rearrange("(j p) -> j p", p=P))
+        for g in range(KG):
+            load_h(g, 1)
+        nc.sync.dma_start(out=cw[:].bitcast(I32), in_=c_words.rearrange("g p n -> p g n").bitcast(I32))
+        nc.sync.dma_start(out=lw[:].bitcast(I32), in_=l_words.rearrange("g p n -> p g n").bitcast(I32))
+        load_scales(nc.sync, cs, c_scales)
+        load_scales(nc.sync, ls, l_scales)
+
+        idle_ps = psum.tile([P, 512], F32, tag="bank", name="idle_ps")
+        for i in range(8):
+            nc.tensor.matmul(out=idle_ps[:], lhsT=idle[:, 0:P], rhs=idle[:], start=True, stop=True)
+
+        xt, zt, zc, zs, ox = {}, {}, {}, {}, {}
+        bank = {}
+
+        def order_b(g, half):
+            c0 = half * 512
+            nc.vector.tensor_copy(
+                out=bw[:, g, :].rearrange("p (t c b) -> p t c b", t=4, b=2)[:, :, half * P : (half + 1) * P, :],
+                in_=bw_raw[:, g, 2 * c0 : 2 * c0 + 1024].rearrange("p (c t b) -> p t c b", t=4, b=2),
+            )
+
+        def order_bs(g, half):
+            nc.vector.tensor_copy(
+                out=bs[:, g, :].rearrange("p (t c) -> p t c", t=4)[:, :, half * P : (half + 1) * P],
+                in_=bs_raw[:, g, half * 512 : (half + 1) * 512].rearrange("p (c t) -> p t c", t=4),
+            )
+
+        def e_pass(h, fg, t, g):
+            if g == 0:
+                e_ps = psum.tile([P, NH], F32, tag="bank", name="e_ps")
+                bank[h, fg, t] = e_ps
+            c0 = t * 256 + fg * P
+            nc.tensor.matmul_mx(
+                out=bank[h, fg, t][:],
+                lhsT=bw[:, g, 2 * c0 : 2 * c0 + 2 * P].bitcast(FP4X4),
+                lhsT_scale=bs[:, g, c0 : c0 + P],
+                rhs=hw[:, g, 2 * NH * h : 2 * NH * (h + 1)].bitcast(FP4X4),
+                rhs_scale=hs[:, g, NH * h : NH * (h + 1)],
+                start=(g == 0),
+                stop=(g == KG - 1),
+            )
+
+        def tanh_e(h, fg, t):
+            if t == 0:
+                x = keep.tile([P, 4, NH], F32, name="x%d%d" % (h, fg))
+                xt[h, fg] = x
+            c = fg * 4 + t
+            nc.scalar.activation(
+                out=xt[h, fg][:, t, :], in_=bank[h, fg, t][:], func=ACT.Tanh, bias=neg_bench[:, c : c + 1], scale=1.0
+            )
+
+        def make_z(h, fg):
+            z = keep.tile([P, NH, 4], BF16, name="z%d%d" % (h, fg), align_bytes=64)
+            zt[h, fg] = z
+            nc.vector.tensor_tensor(
+                out=z[:],
+                in0=xt[h, fg][:].rearrange("p t n -> p n t"),
+                in1=vol_b[:, fg : fg + 1, :].to_broadcast([P, NH, 4]),
+                op=ALU.mult,
+            )
+
+        def quantise_z(h, fg):
+            codes = keep.tile([P, NH], U32, name="zc%d%d" % (h, fg), align_bytes=64)
+            scales = keep.tile([P, NH], U8, name="zs%d%d" % (h, fg), align_bytes=64)
+            zc[h, fg], zs[h, fg] = codes, scales
+            nc.vector.quantize_mx(
+                out=codes[:].bitcast(FP8X4), scales=scales[:], in_=zt[h, fg][:].rearrange("p n t -> p (n t)")
+            )
+
+        def own_x(h, fg, t):
+            if t == 0:
+                o = keep.tile([P, 4, NH], F32, name="ox%d%d" % (h, fg))
+                ox[h, fg] = o
+            c = fg * 4 + t
+            nc.vector.tensor_scalar(
+                out=ox[h, fg][:, t, :], in0=xt[h, fg][:, t, :], scalar1=own_f[:, c : c + 1], scalar2=None, op0=ALU.mult
+            )
+
+        ybank, tbank, ubank, xs, us = {}, {}, {}, {}, {}
+
+        def z_pass(out, j, fg, words, scales, n0):
+            h, c0 = j // 4, P * (j % 4)
+            nc.tensor.matmul_mx(
+                out=out,
+                lhsT=zc[h, fg][:, c0 : c0 + P].bitcast(FP8X4),
+                lhsT_scale=zs[h, fg][:, c0 : c0 + P],
+                rhs=words[:, fg, 2 * n0 : 2 * n0 + 1024].bitcast(FP4X4),
+                rhs_scale=scales[:, fg, n0 : n0 + 512],
+                start=(fg == 0),
+                stop=(fg == FG - 1),
+            )
+
+        def y_mm(j):
+            y_ps = psum.tile([P, DIRECTIONS], F32, tag="bank", name="y_ps")
+            ybank[j] = y_ps
+            for fg in range(FG):
+                z_pass(y_ps[:], j, fg, lw, ls, 0)
+
+        def y_square(j):
+            sq = work.tile([P, DIRECTIONS], BF16, name="sq", bufs=2)
+            nc.scalar.activation(
+                out=sq[:], in_=ybank[j][:], func=ACT.Square, scale=DIRECTIONS**-0.5, accum_out=ms[:, j : j + 1]
+            )
+            nc.gpsimd.tensor_tensor(out=var[:, j : j + 1], in0=ms[:, j : j + 1], in1=spec_f[:, j : j + 1], op=ALU.add)
+            nc.gpsimd.tensor_tensor(out=rs[:, j : j + 1], in0=var[:, j : j + 1], in1=minus_half[:], op=ALU.pow)
+
+        def y_out(j):
+            y_sb = work.tile([P, DIRECTIONS], F32, name="y_sb")
+            nc.scalar.activation(out=y_sb[:], in_=ybank[j][:], func=ACT.Copy, scale=rs[:, j : j + 1])
+            nc.sync.dma_start(out=out_1[P * j : P * (j + 1), :], in_=y_sb[:])
+
+        def turn(j):
+            h, c0 = j // 4, P * (j % 4)
+            for fg in range(FG):
+                t_ps = psum.tile([P, 4, P], F32, tag="bank", name="t_ps")
+                tbank[j, fg] = t_ps
+                for t in range(4):
+                    nc.tensor.transpose(t_ps[:, t, :], ox[h, fg][:, t, c0 : c0 + P], ident[:])
+
+        def turn_out(j):
+            for fg in range(FG):
+                o = work.tile([P, 512], F32, name="xs", bufs=8)
+                xs[j, fg] = o
+                nc.scalar.activation(
+                    out=o[:].rearrange("p (m t) -> p m t", t=4),
+                    in_=tbank[j, fg][:].rearrange("p t m -> p m t"),
+                    func=ACT.Copy,
+                    scale=rs[:, j : j + 1],
+                )
+
+        def u_mm(j):
+            for half in range(2):
+                u_ps = psum.tile([P, 512], F32, tag="bank", name="u_ps")
+                ubank[j, half] = u_ps
+                for fg in range(FG):
+                    z_pass(u_ps[:], j, fg, cw, cs, 512 * half)
+
+        def u_out(j):
+            u_sb = work.tile([P, FACTORS], F32, name="u_sb")
+            for half in range(2):
+                width = 256 if j == TILES - 1 and half == 1 else 512
+                for c0 in range(0, 512, width):
+                    cols = slice(512 * half + c0, 512 * half + c0 + width)
+                    nc.vector.scalar_tensor_tensor(
+                        out=u_sb[:, cols],
+                        in0=ubank[j, half][:, c0 : c0 + width],
+                        scalar=rs[:, j : j + 1],
+                        in1=xs[j, half][:, c0 : c0 + width],
+                        op0=ALU.mult,
+                        op1=ALU.add,
+                    )
+                    nc.sync.dma_start(out=out_0[P * j : P * (j + 1), cols], in_=u_sb[:, cols])
+
+        nc.gpsimd.tensor_scalar(
+            out=neg_bench[:], in0=bench_b[:].rearrange("p g t -> p (g t)"), scalar1=-1.0, scalar2=0.0, op0=ALU.mult, op1=ALU.add
+        )
+        nc.gpsimd.tensor_copy(out=own_f[:], in_=own_b[:].rearrange("p g t -> p (g t)"))
+        for g in range(KG):
+            for fg in range(FG):
+                order_b(g, fg)
+                order_bs(g, fg)
+                for t in range(4):
+                    e_pass(0, fg, t, g)
+        for fg in range(FG):
+            for t in range(4):
+                tanh_e(0, fg, t)
+
+        make_z(0, 0)
+        own_x(0, 0, 0)
+        quantise_z(0, 0)
+        make_z(0, 1)
+        own_x(0, 0, 1)
+        quantise_z(0, 1)
+        for fg, t in ((0, 2), (0, 3), (1, 0), (1, 1), (1, 2), (1, 3)):
+            own_x(0, fg, t)
+
+        def e_tile(h, fg, t):
+            for g in range(KG):
+                e_pass(h, fg, t, g)
+
+        for fg, t in ((0, 0), (0, 1), (0, 2), (0, 3), (1, 0), (1, 1)):
+            e_tile(1, fg, t)
+            tanh_e(1, fg, t)
+        spec_ps = psum.tile([P, P], BF16, tag="bank", name="spec_ps")
+        nc.tensor.transpose(spec_ps[:], spec_rows[:], ident_b[:])
+        nc.scalar.copy(out=spec_f[:], in_=spec_ps[:, 0:TILES])
+        for j in range(4):
+            y_mm(j)
+            y_square(j)
+        e_tile(1, 1, 2)
+        e_tile(1, 1, 3)
+        tanh_e(1, 1, 2)
+        y_out(0)
+        tanh_e(1, 1, 3)
+        for j in range(1, 4):
+            y_out(j)
+
+        make_z(1, 0)
+        quantise_z(1, 0)
+        make_z(1, 1)
+        own_x(1, 0, 0)
+        quantise_z(1, 1)
+
+        turn(0)
+        turn(1)
+        turn_out(0)
+        turn_out(1)
+        u_mm(0)
+        u_out(0)
+        u_mm(1)
+        u_out(1)
+        own_x(1, 0, 1)
+        own_x(1, 0, 2)
+        own_x(1, 0, 3)
+        turn(2)
+        turn(3)
+        turn_out(2)
+        turn_out(3)
+        u_mm(2)
+        u_out(2)
+        own_x(1, 1, 0)
+        own_x(1, 1, 1)
+        u_mm(3)
+        u_out(3)
+        own_x(1, 1, 2)
+        own_x(1, 1, 3)
+        for j in range(4, 8):
+            y_mm(j)
+            y_square(j)
+        turn(4)
+        turn(5)
+        for j in range(4, 8):
+            y_out(j)
+        turn_out(4)
+        turn_out(5)
+        u_mm(4)
+        u_out(4)
+        u_mm(5)
+        u_out(5)
+        turn(6)
+        turn(7)
+        turn_out(6)
+        turn_out(7)
+        u_mm(6)
+        u_out(6)
+        u_mm(7)
+        u_out(7)

@@ -48,12 +48,11 @@ def tile_stressed_factor_response_f2_kernel(
         vol_b = keep.tile([P, FG, 4], BF16, name="vol_b")
         own_b = keep.tile([P, FG, 4], BF16, name="own_b")
         neg_bench = keep.tile([P, FG * 4], F32, name="neg_bench")
-        own_f = keep.tile([P, FG * 4], F32, name="own_f")
         spec_rows = keep.tile([P, P], BF16, name="spec_rows")
         spec_f = keep.tile([P, TILES], F32, name="spec_f")
         ident_b = keep.tile([P, P], BF16, name="ident_b")
         ident = keep.tile([P, P], F32, name="ident")
-        minus_half = keep.tile([P, 1], F32, name="minus_half")
+        minus_half = keep.tile([P, 2], F32, name="minus_half")
         ms = keep.tile([P, TILES], F32, name="ms")
         var = keep.tile([P, TILES], F32, name="var")
         rs = keep.tile([P, TILES], F32, name="rs")
@@ -63,8 +62,8 @@ def tile_stressed_factor_response_f2_kernel(
         def flat_i32(t):
             return t[:].rearrange("p g n -> p (g n)").bitcast(I32)
 
-        def load_scales(queue, plane, src):
-            for q in range(4):
+        def load_scales(plane, src, queues):
+            for q, queue in enumerate(queues):
                 queue.dma_start(
                     out=plane[32 * q : 32 * q + 4, :, :].bitcast(I32),
                     in_=src[:, 4 * q : 4 * q + 4, :].rearrange("g r n -> r g n").bitcast(I32),
@@ -73,16 +72,10 @@ def tile_stressed_factor_response_f2_kernel(
         def by_factor(v):
             return v.rearrange("(g p t) -> p g t", g=FG, t=4)
 
+        nc.vector.memset(flat_i32(hs), 0)
         nc.vector.memset(flat_i32(bs_raw), 0)
         nc.vector.memset(warm[:], 0.0)
         nc.gpsimd.memset(idle[:], 0.0)
-        nc.gpsimd.memset(flat_i32(hs), 0)
-        nc.gpsimd.memset(spec_rows[:], 0.0)
-        nc.gpsimd.memset(flat_i32(cs), 0)
-        nc.gpsimd.memset(flat_i32(ls), 0)
-        nc.gpsimd.memset(minus_half[:], -0.5)
-        make_identity(nc, ident[:])
-        make_identity(nc, ident_b[:])
 
         def load_b(g):
             nc.sync.dma_start(out=bw_raw[:, g, :].bitcast(I32), in_=b_words[g].bitcast(I32))
@@ -93,22 +86,29 @@ def tile_stressed_factor_response_f2_kernel(
 
         load_b(0)
         load_h(0, 0)
-        load_scales(nc.sync, bs_raw, b_scales)
-        load_scales(nc.sync, hs, h_scales)
+        load_scales(hs, h_scales, (nc.gpsimd, nc.gpsimd, nc.sync, nc.sync))
+        load_scales(bs_raw, b_scales, (nc.sync,) * 4)
+        nc.gpsimd.memset(spec_rows[:], 0.0)
+        nc.gpsimd.memset(flat_i32(cs), 0)
+        nc.gpsimd.memset(flat_i32(ls), 0)
+        nc.gpsimd.memset(minus_half[:], -0.5)
+        make_identity(nc, ident[:])
+        make_identity(nc, ident_b[:])
         nc.scalar.activation(out=warm[:], in_=warm[:], func=ACT.Tanh)
         for g in range(1, KG):
             load_b(g)
             load_h(g, 0)
-        nc.gpsimd.dma_start(out=bench_b[:], in_=by_factor(bench))
-        nc.gpsimd.dma_start(out=vol_b[:], in_=by_factor(vol))
-        nc.gpsimd.dma_start(out=own_b[:], in_=by_factor(own))
-        nc.gpsimd.dma_start(out=spec_rows[0:TILES, :], in_=spec.rearrange("(j p) -> j p", p=P))
+            if g == 1:
+                nc.scalar.dma_start(out=bench_b[:], in_=by_factor(bench))
+                nc.scalar.dma_start(out=vol_b[:], in_=by_factor(vol))
+                nc.scalar.dma_start(out=own_b[:], in_=by_factor(own))
+                nc.scalar.dma_start(out=spec_rows[0:TILES, :], in_=spec.rearrange("(j p) -> j p", p=P))
         for g in range(KG):
             load_h(g, 1)
         nc.sync.dma_start(out=cw[:].bitcast(I32), in_=c_words.rearrange("g p n -> p g n").bitcast(I32))
         nc.sync.dma_start(out=lw[:].bitcast(I32), in_=l_words.rearrange("g p n -> p g n").bitcast(I32))
-        load_scales(nc.sync, cs, c_scales)
-        load_scales(nc.sync, ls, l_scales)
+        load_scales(cs, c_scales, (nc.sync,) * 4)
+        load_scales(ls, l_scales, (nc.sync,) * 4)
 
         idle_ps = psum.tile([P, 512], F32, tag="bank", name="idle_ps")
         for i in range(8):
@@ -157,12 +157,13 @@ def tile_stressed_factor_response_f2_kernel(
         def make_z(h, fg):
             z = keep.tile([P, NH, 4], BF16, name="z%d%d" % (h, fg), align_bytes=64)
             zt[h, fg] = z
-            nc.vector.tensor_tensor(
-                out=z[:],
-                in0=xt[h, fg][:].rearrange("p t n -> p n t"),
-                in1=vol_b[:, fg : fg + 1, :].to_broadcast([P, NH, 4]),
-                op=ALU.mult,
-            )
+            for c in range(0, NH, P):
+                nc.vector.tensor_tensor(
+                    out=z[:, c : c + P, :],
+                    in0=xt[h, fg][:, :, c : c + P].rearrange("p t n -> p n t"),
+                    in1=vol_b[:, fg : fg + 1, :].to_broadcast([P, P, 4]),
+                    op=ALU.mult,
+                )
 
         def quantise_z(h, fg):
             codes = keep.tile([P, NH], U32, name="zc%d%d" % (h, fg), align_bytes=64)
@@ -178,7 +179,7 @@ def tile_stressed_factor_response_f2_kernel(
                 ox[h, fg] = o
             c = fg * 4 + t
             nc.vector.tensor_scalar(
-                out=ox[h, fg][:, t, :], in0=xt[h, fg][:, t, :], scalar1=own_f[:, c : c + 1], scalar2=None, op0=ALU.mult
+                out=ox[h, fg][:, t, :], in0=xt[h, fg][:, t, :], scalar1=own_b[:, fg, t : t + 1], scalar2=None, op0=ALU.mult
             )
 
         ybank, tbank, ubank, xs, us = {}, {}, {}, {}, {}
@@ -206,8 +207,10 @@ def tile_stressed_factor_response_f2_kernel(
             nc.scalar.activation(
                 out=sq[:], in_=ybank[j][:], func=ACT.Square, scale=DIRECTIONS**-0.5, accum_out=ms[:, j : j + 1]
             )
-            nc.gpsimd.tensor_tensor(out=var[:, j : j + 1], in0=ms[:, j : j + 1], in1=spec_f[:, j : j + 1], op=ALU.add)
-            nc.gpsimd.tensor_tensor(out=rs[:, j : j + 1], in0=var[:, j : j + 1], in1=minus_half[:], op=ALU.pow)
+            if j % 2:
+                pair = slice(j - 1, j + 1)
+                nc.gpsimd.tensor_tensor(out=var[:, pair], in0=ms[:, pair], in1=spec_f[:, pair], op=ALU.add)
+                nc.gpsimd.tensor_tensor(out=rs[:, pair], in0=var[:, pair], in1=minus_half[:], op=ALU.pow)
 
         def y_out(j):
             y_sb = work.tile([P, DIRECTIONS], F32, name="y_sb")
@@ -256,10 +259,7 @@ def tile_stressed_factor_response_f2_kernel(
                     )
                     nc.sync.dma_start(out=out_0[P * j : P * (j + 1), cols], in_=u_sb[:, cols])
 
-        nc.gpsimd.tensor_scalar(
-            out=neg_bench[:], in0=bench_b[:].rearrange("p g t -> p (g t)"), scalar1=-1.0, scalar2=0.0, op0=ALU.mult, op1=ALU.add
-        )
-        nc.gpsimd.tensor_copy(out=own_f[:], in_=own_b[:].rearrange("p g t -> p (g t)"))
+        nc.scalar.activation(out=neg_bench[:], in_=bench_b[:].rearrange("p g t -> p (g t)"), func=ACT.Copy, scale=-1.0)
         for g in range(KG):
             for fg in range(FG):
                 order_b(g, fg)

@@ -40,6 +40,8 @@ def tile_stressed_factor_response_f2_kernel(
         bs = keep.tile([P, KG, FACTORS], U8, name="bs", align_bytes=64)
         hw = keep.tile([P, KG, 2 * PORTFOLIOS], U8, name="hw", align_bytes=64)
         hs = keep.tile([P, KG, PORTFOLIOS], U8, name="hs", align_bytes=64)
+        cw_raw = keep.tile([P, FG, 2 * FACTORS], U8, name="cw_raw", align_bytes=64)
+        cs_raw = keep.tile([P, FG, FACTORS], U8, name="cs_raw", align_bytes=64)
         cw = keep.tile([P, FG, 2 * FACTORS], U8, name="cw", align_bytes=64)
         cs = keep.tile([P, FG, FACTORS], U8, name="cs", align_bytes=64)
         lw = keep.tile([P, FG, 2 * DIRECTIONS], U8, name="lw", align_bytes=64)
@@ -52,9 +54,8 @@ def tile_stressed_factor_response_f2_kernel(
         spec_f = keep.tile([P, TILES], F32, name="spec_f")
         ident_b = keep.tile([P, P], BF16, name="ident_b")
         ident = keep.tile([P, P], F32, name="ident")
-        minus_half = keep.tile([P, 2], F32, name="minus_half")
+        one = keep.tile([P, 1], F32, name="one")
         ms = keep.tile([P, TILES], F32, name="ms")
-        var = keep.tile([P, TILES], F32, name="var")
         rs = keep.tile([P, TILES], F32, name="rs")
         warm = keep.tile([P, 1], F32, name="warm")
         idle = keep.tile([P, 512], BF16, name="idle")
@@ -62,20 +63,21 @@ def tile_stressed_factor_response_f2_kernel(
         def flat_i32(t):
             return t[:].rearrange("p g n -> p (g n)").bitcast(I32)
 
-        def load_scales(plane, src, queues):
+        def load_scales(plane, src, g0, g1, queues):
             for q, queue in enumerate(queues):
                 queue.dma_start(
-                    out=plane[32 * q : 32 * q + 4, :, :].bitcast(I32),
-                    in_=src[:, 4 * q : 4 * q + 4, :].rearrange("g r n -> r g n").bitcast(I32),
+                    out=plane[32 * q : 32 * q + 4, g0:g1, :].bitcast(I32),
+                    in_=src[g0:g1, 4 * q : 4 * q + 4, :].rearrange("g r n -> r g n").bitcast(I32),
                 )
 
         def by_factor(v):
             return v.rearrange("(g p t) -> p g t", g=FG, t=4)
 
-        nc.vector.memset(flat_i32(hs), 0)
-        nc.vector.memset(flat_i32(bs_raw), 0)
-        nc.vector.memset(warm[:], 0.0)
         nc.gpsimd.memset(idle[:], 0.0)
+        for g in (slice(0, 1), slice(1, KG)):
+            nc.vector.memset(hs[:, g, :].rearrange("p g n -> p (g n)").bitcast(I32), 0)
+            nc.vector.memset(bs_raw[:, g, :].rearrange("p g n -> p (g n)").bitcast(I32), 0)
+        nc.vector.memset(warm[:], 0.0)
 
         def load_b(g):
             nc.sync.dma_start(out=bw_raw[:, g, :].bitcast(I32), in_=b_words[g].bitcast(I32))
@@ -86,35 +88,38 @@ def tile_stressed_factor_response_f2_kernel(
 
         load_b(0)
         load_h(0, 0)
-        load_scales(hs, h_scales, (nc.gpsimd, nc.gpsimd, nc.sync, nc.sync))
-        load_scales(bs_raw, b_scales, (nc.sync,) * 4)
+        load_scales(hs, h_scales, 0, KG, (nc.gpsimd, nc.gpsimd, nc.sync, nc.sync))
+        load_scales(bs_raw, b_scales, 0, KG, (nc.sync,) * 4)
+        nc.gpsimd.dma_start(out=bench_b[:], in_=by_factor(bench))
         nc.gpsimd.memset(spec_rows[:], 0.0)
-        nc.gpsimd.memset(flat_i32(cs), 0)
+        nc.gpsimd.memset(flat_i32(cs_raw), 0)
         nc.gpsimd.memset(flat_i32(ls), 0)
-        nc.gpsimd.memset(minus_half[:], -0.5)
+        nc.gpsimd.memset(one[:], 1.0)
         make_identity(nc, ident[:])
         make_identity(nc, ident_b[:])
         nc.scalar.activation(out=warm[:], in_=warm[:], func=ACT.Tanh)
-        for g in range(1, KG):
+        load_b(1)
+        load_h(1, 0)
+        nc.scalar.dma_start(out=vol_b[:], in_=by_factor(vol))
+        nc.scalar.dma_start(out=own_b[:], in_=by_factor(own))
+        nc.scalar.dma_start(out=spec_rows[0:TILES, :], in_=spec.rearrange("(j p) -> j p", p=P))
+        for g in range(2, KG):
             load_b(g)
             load_h(g, 0)
-            if g == 1:
-                nc.scalar.dma_start(out=bench_b[:], in_=by_factor(bench))
-                nc.scalar.dma_start(out=vol_b[:], in_=by_factor(vol))
-                nc.scalar.dma_start(out=own_b[:], in_=by_factor(own))
-                nc.scalar.dma_start(out=spec_rows[0:TILES, :], in_=spec.rearrange("(j p) -> j p", p=P))
-        for g in range(KG):
-            load_h(g, 1)
-        nc.sync.dma_start(out=cw[:].bitcast(I32), in_=c_words.rearrange("g p n -> p g n").bitcast(I32))
+        nc.sync.dma_start(out=cw_raw[:].bitcast(I32), in_=c_words.rearrange("g p n -> p g n").bitcast(I32))
+        load_scales(cs_raw, c_scales, 0, FG, (nc.sync,) * 4)
+        half_1 = slice(2 * NH, 4 * NH)
+        nc.sync.dma_start(
+            out=hw[:, :, half_1].bitcast(I32), in_=h_words[:, :, half_1].rearrange("g p n -> p g n").bitcast(I32)
+        )
         nc.sync.dma_start(out=lw[:].bitcast(I32), in_=l_words.rearrange("g p n -> p g n").bitcast(I32))
-        load_scales(cs, c_scales, (nc.sync,) * 4)
-        load_scales(ls, l_scales, (nc.sync,) * 4)
+        load_scales(ls, l_scales, 0, FG, (nc.sync,) * 4)
 
         idle_ps = psum.tile([P, 512], F32, tag="bank", name="idle_ps")
         for i in range(8):
             nc.tensor.matmul(out=idle_ps[:], lhsT=idle[:, 0:P], rhs=idle[:], start=True, stop=True)
 
-        xt, zt, zc, zs, ox = {}, {}, {}, {}, {}
+        xt, zt, zc, zs = {}, {}, {}, {}
         bank = {}
 
         def order_b(g, half):
@@ -128,6 +133,18 @@ def tile_stressed_factor_response_f2_kernel(
             nc.vector.tensor_copy(
                 out=bs[:, g, :].rearrange("p (t c) -> p t c", t=4)[:, :, half * P : (half + 1) * P],
                 in_=bs_raw[:, g, half * 512 : (half + 1) * 512].rearrange("p (c t) -> p t c", t=4),
+            )
+
+        def order_c(g):
+            nc.vector.tensor_copy(
+                out=cw[:, g, :].rearrange("p (t c b) -> p t c b", t=4, b=2),
+                in_=cw_raw[:, g, :].rearrange("p (c t b) -> p t c b", t=4, b=2),
+            )
+
+        def order_cs(g):
+            nc.vector.tensor_copy(
+                out=cs[:, g, :].rearrange("p (t c) -> p t c", t=4),
+                in_=cs_raw[:, g, :].rearrange("p (c t) -> p t c", t=4),
             )
 
         def e_pass(h, fg, t, g):
@@ -157,13 +174,12 @@ def tile_stressed_factor_response_f2_kernel(
         def make_z(h, fg):
             z = keep.tile([P, NH, 4], BF16, name="z%d%d" % (h, fg), align_bytes=64)
             zt[h, fg] = z
-            for c in range(0, NH, P):
-                nc.vector.tensor_tensor(
-                    out=z[:, c : c + P, :],
-                    in0=xt[h, fg][:, :, c : c + P].rearrange("p t n -> p n t"),
-                    in1=vol_b[:, fg : fg + 1, :].to_broadcast([P, P, 4]),
-                    op=ALU.mult,
-                )
+            nc.vector.tensor_tensor(
+                out=z[:],
+                in0=xt[h, fg][:].rearrange("p t n -> p n t"),
+                in1=vol_b[:, fg : fg + 1, :].to_broadcast([P, NH, 4]),
+                op=ALU.mult,
+            )
 
         def quantise_z(h, fg):
             codes = keep.tile([P, NH], U32, name="zc%d%d" % (h, fg), align_bytes=64)
@@ -173,34 +189,31 @@ def tile_stressed_factor_response_f2_kernel(
                 out=codes[:].bitcast(FP8X4), scales=scales[:], in_=zt[h, fg][:].rearrange("p n t -> p (n t)")
             )
 
-        def own_x(h, fg, t):
-            if t == 0:
-                o = keep.tile([P, 4, NH], F32, name="ox%d%d" % (h, fg))
-                ox[h, fg] = o
-            c = fg * 4 + t
-            nc.vector.tensor_scalar(
-                out=ox[h, fg][:, t, :], in0=xt[h, fg][:, t, :], scalar1=own_b[:, fg, t : t + 1], scalar2=None, op0=ALU.mult
-            )
-
-        ybank, tbank, ubank, xs, us = {}, {}, {}, {}, {}
-
-        def z_pass(out, j, fg, words, scales, n0):
-            h, c0 = j // 4, P * (j % 4)
-            nc.tensor.matmul_mx(
-                out=out,
-                lhsT=zc[h, fg][:, c0 : c0 + P].bitcast(FP8X4),
-                lhsT_scale=zs[h, fg][:, c0 : c0 + P],
-                rhs=words[:, fg, 2 * n0 : 2 * n0 + 1024].bitcast(FP4X4),
-                rhs_scale=scales[:, fg, n0 : n0 + 512],
-                start=(fg == 0),
-                stop=(fg == FG - 1),
-            )
+        ybank, tbank, ubank, vt, us = {}, {}, {}, {}, {}
 
         def y_mm(j):
+            h, c0 = j // 4, P * (j % 4)
             y_ps = psum.tile([P, DIRECTIONS], F32, tag="bank", name="y_ps")
             ybank[j] = y_ps
-            for fg in range(FG):
-                z_pass(y_ps[:], j, fg, lw, ls, 0)
+            for g in range(FG):
+                nc.tensor.matmul_mx(
+                    out=y_ps[:],
+                    lhsT=zc[h, g][:, c0 : c0 + P].bitcast(FP8X4),
+                    lhsT_scale=zs[h, g][:, c0 : c0 + P],
+                    rhs=lw[:, g, :].bitcast(FP4X4),
+                    rhs_scale=ls[:, g, :],
+                    start=(g == 0),
+                    stop=(g == FG - 1),
+                )
+
+        def inverse_risk(j):
+            nc.scalar.activation(
+                out=rs[:, j : j + 1],
+                in_=ms[:, j : j + 1],
+                func=ACT.Abs_reciprocal_sqrt,
+                bias=spec_f[:, j : j + 1],
+                scale=1.0,
+            )
 
         def y_square(j):
             sq = work.tile([P, DIRECTIONS], BF16, name="sq", bufs=2)
@@ -208,56 +221,68 @@ def tile_stressed_factor_response_f2_kernel(
                 out=sq[:], in_=ybank[j][:], func=ACT.Square, scale=DIRECTIONS**-0.5, accum_out=ms[:, j : j + 1]
             )
             if j % 2:
-                pair = slice(j - 1, j + 1)
-                nc.gpsimd.tensor_tensor(out=var[:, pair], in0=ms[:, pair], in1=spec_f[:, pair], op=ALU.add)
-                nc.gpsimd.tensor_tensor(out=rs[:, pair], in0=var[:, pair], in1=minus_half[:], op=ALU.pow)
+                inverse_risk(j - 1)
+                inverse_risk(j)
 
-        def y_out(j):
+        def scaled(engine, out, in_, j):
+            if engine is nc.scalar:
+                nc.scalar.activation(out=out, in_=in_, func=ACT.Copy, scale=rs[:, j : j + 1])
+            else:
+                nc.vector.tensor_scalar(out=out, in0=in_, scalar1=rs[:, j : j + 1], scalar2=None, op0=ALU.mult)
+
+        def y_out(j, engine):
             y_sb = work.tile([P, DIRECTIONS], F32, name="y_sb")
-            nc.scalar.activation(out=y_sb[:], in_=ybank[j][:], func=ACT.Copy, scale=rs[:, j : j + 1])
+            scaled(engine, y_sb[:], ybank[j][:], j)
             nc.sync.dma_start(out=out_1[P * j : P * (j + 1), :], in_=y_sb[:])
 
-        def turn(j):
-            h, c0 = j // 4, P * (j % 4)
-            for fg in range(FG):
-                t_ps = psum.tile([P, 4, P], F32, tag="bank", name="t_ps")
-                tbank[j, fg] = t_ps
-                for t in range(4):
-                    nc.tensor.transpose(t_ps[:, t, :], ox[h, fg][:, t, c0 : c0 + P], ident[:])
-
-        def turn_out(j):
-            for fg in range(FG):
-                o = work.tile([P, 512], F32, name="xs", bufs=8)
-                xs[j, fg] = o
-                nc.scalar.activation(
-                    out=o[:].rearrange("p (m t) -> p m t", t=4),
-                    in_=tbank[j, fg][:].rearrange("p t m -> p m t"),
-                    func=ACT.Copy,
-                    scale=rs[:, j : j + 1],
+        def u_mm(h, fg, t):
+            u_ps = psum.tile([P, NH], F32, tag="bank", name="u_ps")
+            ubank[h, fg, t] = u_ps
+            c0 = t * 256 + fg * P
+            for g in range(FG):
+                nc.tensor.matmul_mx(
+                    out=u_ps[:],
+                    lhsT=cw[:, g, 2 * c0 : 2 * c0 + 2 * P].bitcast(FP4X4),
+                    lhsT_scale=cs[:, g, c0 : c0 + P],
+                    rhs=zc[h, g][:].bitcast(FP8X4),
+                    rhs_scale=zs[h, g][:],
+                    start=(g == 0),
+                    stop=(g == FG - 1),
                 )
 
-        def u_mm(j):
-            for half in range(2):
-                u_ps = psum.tile([P, 512], F32, tag="bank", name="u_ps")
-                ubank[j, half] = u_ps
-                for fg in range(FG):
-                    z_pass(u_ps[:], j, fg, cw, cs, 512 * half)
+        def add_own(h, fg, t):
+            if t == 0:
+                v = keep.tile([P, 4, NH], F32, name="v%d%d" % (h, fg))
+                vt[h, fg] = v
+            nc.vector.scalar_tensor_tensor(
+                out=vt[h, fg][:, t, :],
+                in0=xt[h, fg][:, t, :],
+                scalar=own_b[:, fg, t : t + 1],
+                in1=ubank[h, fg, t][:],
+                op0=ALU.mult,
+                op1=ALU.add,
+            )
 
-        def u_out(j):
-            u_sb = work.tile([P, FACTORS], F32, name="u_sb")
-            for half in range(2):
-                width = 256 if j == TILES - 1 and half == 1 else 512
-                for c0 in range(0, 512, width):
-                    cols = slice(512 * half + c0, 512 * half + c0 + width)
-                    nc.vector.scalar_tensor_tensor(
-                        out=u_sb[:, cols],
-                        in0=ubank[j, half][:, c0 : c0 + width],
-                        scalar=rs[:, j : j + 1],
-                        in1=xs[j, half][:, c0 : c0 + width],
-                        op0=ALU.mult,
-                        op1=ALU.add,
-                    )
-                    nc.sync.dma_start(out=out_0[P * j : P * (j + 1), cols], in_=u_sb[:, cols])
+        def turn(h, fg):
+            for i in range(4):
+                t_ps = psum.tile([P, 4, P], F32, tag="bank", name="t_ps")
+                tbank[4 * h + i, fg] = t_ps
+            for t in range(4):
+                for i in range(4):
+                    nc.tensor.transpose(tbank[4 * h + i, fg][:, t, :], vt[h, fg][:, t, P * i : P * (i + 1)], ident[:])
+
+        def u_out(j, fg, engine):
+            if fg == 0:
+                u_sb = work.tile([P, FACTORS], F32, name="u_sb", bufs=8)
+                us[j] = u_sb
+            cols = slice(512 * fg, 512 * (fg + 1))
+            scaled(
+                engine,
+                us[j][:, cols].rearrange("p (m t) -> p m t", t=4),
+                tbank[j, fg][:].rearrange("p t m -> p m t"),
+                j,
+            )
+            nc.sync.dma_start(out=out_0[P * j : P * (j + 1), cols], in_=us[j][:, cols])
 
         nc.scalar.activation(out=neg_bench[:], in_=bench_b[:].rearrange("p g t -> p (g t)"), func=ACT.Copy, scale=-1.0)
         for g in range(KG):
@@ -266,87 +291,67 @@ def tile_stressed_factor_response_f2_kernel(
                 order_bs(g, fg)
                 for t in range(4):
                     e_pass(0, fg, t, g)
+        for g in range(FG):
+            order_c(g)
+            order_cs(g)
         for fg in range(FG):
             for t in range(4):
                 tanh_e(0, fg, t)
-
         make_z(0, 0)
-        own_x(0, 0, 0)
-        quantise_z(0, 0)
         make_z(0, 1)
-        own_x(0, 0, 1)
+        quantise_z(0, 0)
         quantise_z(0, 1)
-        for fg, t in ((0, 2), (0, 3), (1, 0), (1, 1), (1, 2), (1, 3)):
-            own_x(0, fg, t)
+        for fg in range(FG):
+            for t in range(4):
+                for g in range(KG):
+                    e_pass(1, fg, t, g)
+                tanh_e(1, fg, t)
+        make_z(1, 0)
 
-        def e_tile(h, fg, t):
-            for g in range(KG):
-                e_pass(h, fg, t, g)
-
-        for fg, t in ((0, 0), (0, 1), (0, 2), (0, 3), (1, 0), (1, 1)):
-            e_tile(1, fg, t)
-            tanh_e(1, fg, t)
         spec_ps = psum.tile([P, P], BF16, tag="bank", name="spec_ps")
         nc.tensor.transpose(spec_ps[:], spec_rows[:], ident_b[:])
         nc.scalar.copy(out=spec_f[:], in_=spec_ps[:, 0:TILES])
-        for j in range(4):
+        nc.scalar.activation(out=one[:], in_=one[:], func=ACT.Abs_reciprocal_sqrt)
+        first, second = range(0, 4), range(4, 8)
+        for j in first:
             y_mm(j)
             y_square(j)
-        e_tile(1, 1, 2)
-        e_tile(1, 1, 3)
-        tanh_e(1, 1, 2)
-        y_out(0)
-        tanh_e(1, 1, 3)
-        for j in range(1, 4):
-            y_out(j)
-
-        make_z(1, 0)
+            if j % 2:
+                y_out(j - 1, nc.scalar)
+                y_out(j, nc.scalar)
+            if j == 1:
+                for t in range(4):
+                    u_mm(0, 0, t)
+                make_z(1, 1)
+                for t in range(4):
+                    add_own(0, 0, t)
         quantise_z(1, 0)
-        make_z(1, 1)
-        own_x(1, 0, 0)
+        for t in range(4):
+            u_mm(0, 1, t)
+            add_own(0, 1, t)
         quantise_z(1, 1)
-
-        turn(0)
-        turn(1)
-        turn_out(0)
-        turn_out(1)
-        u_mm(0)
-        u_out(0)
-        u_mm(1)
-        u_out(1)
-        own_x(1, 0, 1)
-        own_x(1, 0, 2)
-        own_x(1, 0, 3)
-        turn(2)
-        turn(3)
-        turn_out(2)
-        turn_out(3)
-        u_mm(2)
-        u_out(2)
-        own_x(1, 1, 0)
-        own_x(1, 1, 1)
-        u_mm(3)
-        u_out(3)
-        own_x(1, 1, 2)
-        own_x(1, 1, 3)
-        for j in range(4, 8):
+        turn(0, 0)
+        for j in first:
+            u_out(j, 0, nc.scalar)
+        turn(0, 1)
+        for j in first:
+            u_out(j, 1, nc.scalar)
+        for t in range(4):
+            u_mm(1, 0, t)
+            add_own(1, 0, t)
+        for j in second:
             y_mm(j)
             y_square(j)
-        turn(4)
-        turn(5)
-        for j in range(4, 8):
-            y_out(j)
-        turn_out(4)
-        turn_out(5)
-        u_mm(4)
-        u_out(4)
-        u_mm(5)
-        u_out(5)
-        turn(6)
-        turn(7)
-        turn_out(6)
-        turn_out(7)
-        u_mm(6)
-        u_out(6)
-        u_mm(7)
-        u_out(7)
+            if j % 2:
+                y_out(j - 1, nc.scalar)
+                y_out(j, nc.vector)
+        for t in range(4):
+            u_mm(1, 1, t)
+            add_own(1, 1, t)
+            if t == 1:
+                turn(1, 0)
+                for j in second:
+                    u_out(j, 0, nc.scalar)
+        turn(1, 1)
+        for j in second:
+            u_out(j, 1, nc.vector if j % 2 else nc.scalar)

@@ -63,21 +63,26 @@ def tile_stressed_factor_response_f2_kernel(
         def flat_i32(t):
             return t[:].rearrange("p g n -> p (g n)").bitcast(I32)
 
-        def load_scales(plane, src, g0, g1, queues):
-            for q, queue in enumerate(queues):
-                queue.dma_start(
-                    out=plane[32 * q : 32 * q + 4, g0:g1, :].bitcast(I32),
-                    in_=src[g0:g1, 4 * q : 4 * q + 4, :].rearrange("g r n -> r g n").bitcast(I32),
+        def load_scales(plane, src):
+            for q in range(4):
+                nc.sync.dma_start(
+                    out=plane[32 * q : 32 * q + 4, :, :].bitcast(I32),
+                    in_=src[:, 4 * q : 4 * q + 4, :].rearrange("g r n -> r g n").bitcast(I32),
                 )
 
         def by_factor(v):
             return v.rearrange("(g p t) -> p g t", g=FG, t=4)
 
         nc.gpsimd.memset(idle[:], 0.0)
-        for g in (slice(0, 1), slice(1, KG)):
-            nc.vector.memset(hs[:, g, :].rearrange("p g n -> p (g n)").bitcast(I32), 0)
-            nc.vector.memset(bs_raw[:, g, :].rearrange("p g n -> p (g n)").bitcast(I32), 0)
+        nc.vector.memset(flat_i32(hs), 0)
+        nc.gpsimd.memset(flat_i32(bs_raw), 0)
         nc.vector.memset(warm[:], 0.0)
+        nc.gpsimd.memset(flat_i32(cs_raw), 0)
+        nc.gpsimd.memset(spec_rows[:], 0.0)
+        nc.gpsimd.memset(flat_i32(ls), 0)
+        nc.gpsimd.memset(one[:], 1.0)
+        make_identity(nc, ident[:])
+        make_identity(nc, ident_b[:])
 
         def load_b(g):
             nc.sync.dma_start(out=bw_raw[:, g, :].bitcast(I32), in_=b_words[g].bitcast(I32))
@@ -86,37 +91,29 @@ def tile_stressed_factor_response_f2_kernel(
             cols = slice(2 * NH * h, 2 * NH * (h + 1))
             nc.sync.dma_start(out=hw[:, g, cols].bitcast(I32), in_=h_words[g][:, cols].bitcast(I32))
 
+        nc.scalar.activation(out=warm[:], in_=warm[:], func=ACT.Tanh)
         load_b(0)
         load_h(0, 0)
-        load_scales(hs, h_scales, 0, KG, (nc.gpsimd, nc.gpsimd, nc.sync, nc.sync))
-        load_scales(bs_raw, b_scales, 0, KG, (nc.sync,) * 4)
-        nc.gpsimd.dma_start(out=bench_b[:], in_=by_factor(bench))
-        nc.gpsimd.memset(spec_rows[:], 0.0)
-        nc.gpsimd.memset(flat_i32(cs_raw), 0)
-        nc.gpsimd.memset(flat_i32(ls), 0)
-        nc.gpsimd.memset(one[:], 1.0)
-        make_identity(nc, ident[:])
-        make_identity(nc, ident_b[:])
-        nc.scalar.activation(out=warm[:], in_=warm[:], func=ACT.Tanh)
-        load_b(1)
-        load_h(1, 0)
-        nc.scalar.dma_start(out=vol_b[:], in_=by_factor(vol))
-        nc.scalar.dma_start(out=own_b[:], in_=by_factor(own))
-        nc.scalar.dma_start(out=spec_rows[0:TILES, :], in_=spec.rearrange("(j p) -> j p", p=P))
-        for g in range(2, KG):
+        load_scales(hs, h_scales)
+        load_scales(bs_raw, b_scales)
+        for g in range(1, KG):
             load_b(g)
             load_h(g, 0)
+        nc.sync.dma_start(out=bench_b[:], in_=by_factor(bench))
+        nc.sync.dma_start(out=vol_b[:], in_=by_factor(vol))
         nc.sync.dma_start(out=cw_raw[:].bitcast(I32), in_=c_words.rearrange("g p n -> p g n").bitcast(I32))
-        load_scales(cs_raw, c_scales, 0, FG, (nc.sync,) * 4)
         half_1 = slice(2 * NH, 4 * NH)
         nc.sync.dma_start(
             out=hw[:, :, half_1].bitcast(I32), in_=h_words[:, :, half_1].rearrange("g p n -> p g n").bitcast(I32)
         )
+        load_scales(cs_raw, c_scales)
+        nc.sync.dma_start(out=own_b[:], in_=by_factor(own))
+        nc.sync.dma_start(out=spec_rows[0:TILES, :], in_=spec.rearrange("(j p) -> j p", p=P))
         nc.sync.dma_start(out=lw[:].bitcast(I32), in_=l_words.rearrange("g p n -> p g n").bitcast(I32))
-        load_scales(ls, l_scales, 0, FG, (nc.sync,) * 4)
+        load_scales(ls, l_scales)
 
         idle_ps = psum.tile([P, 512], F32, tag="bank", name="idle_ps")
-        for i in range(8):
+        for i in range(14):
             nc.tensor.matmul(out=idle_ps[:], lhsT=idle[:, 0:P], rhs=idle[:], start=True, stop=True)
 
         xt, zt, zc, zs = {}, {}, {}, {}
@@ -235,40 +232,42 @@ def tile_stressed_factor_response_f2_kernel(
             scaled(engine, y_sb[:], ybank[j][:], j)
             nc.sync.dma_start(out=out_1[P * j : P * (j + 1), :], in_=y_sb[:])
 
-        def u_mm(h, fg, t):
+        def u_mm(h, fg, t, n0=0, n1=NH):
             u_ps = psum.tile([P, NH], F32, tag="bank", name="u_ps")
             ubank[h, fg, t] = u_ps
             c0 = t * 256 + fg * P
-            for g in range(FG):
-                nc.tensor.matmul_mx(
-                    out=u_ps[:],
-                    lhsT=cw[:, g, 2 * c0 : 2 * c0 + 2 * P].bitcast(FP4X4),
-                    lhsT_scale=cs[:, g, c0 : c0 + P],
-                    rhs=zc[h, g][:].bitcast(FP8X4),
-                    rhs_scale=zs[h, g][:],
-                    start=(g == 0),
-                    stop=(g == FG - 1),
-                )
+            width = NH if n1 - n0 == NH else P
+            for n in range(n0, n1, width):
+                for g in range(FG):
+                    nc.tensor.matmul_mx(
+                        out=u_ps[:, n : n + width],
+                        lhsT=cw[:, g, 2 * c0 : 2 * c0 + 2 * P].bitcast(FP4X4),
+                        lhsT_scale=cs[:, g, c0 : c0 + P],
+                        rhs=zc[h, g][:, n : n + width].bitcast(FP8X4),
+                        rhs_scale=zs[h, g][:, n : n + width],
+                        start=(g == 0),
+                        stop=(g == FG - 1),
+                    )
 
-        def add_own(h, fg, t):
-            if t == 0:
+        def add_own(h, fg, t, n0=0, n1=NH):
+            if t == 0 and n0 == 0:
                 v = keep.tile([P, 4, NH], F32, name="v%d%d" % (h, fg))
                 vt[h, fg] = v
             nc.vector.scalar_tensor_tensor(
-                out=vt[h, fg][:, t, :],
-                in0=xt[h, fg][:, t, :],
+                out=vt[h, fg][:, t, n0:n1],
+                in0=xt[h, fg][:, t, n0:n1],
                 scalar=own_b[:, fg, t : t + 1],
-                in1=ubank[h, fg, t][:],
+                in1=ubank[h, fg, t][:, n0:n1],
                 op0=ALU.mult,
                 op1=ALU.add,
             )
 
-        def turn(h, fg):
-            for i in range(4):
+        def turn(h, fg, i0=0, i1=4):
+            for i in range(i0, i1):
                 t_ps = psum.tile([P, 4, P], F32, tag="bank", name="t_ps")
                 tbank[4 * h + i, fg] = t_ps
             for t in range(4):
-                for i in range(4):
+                for i in range(i0, i1):
                     nc.tensor.transpose(tbank[4 * h + i, fg][:, t, :], vt[h, fg][:, t, P * i : P * (i + 1)], ident[:])
 
         def u_out(j, fg, engine):
@@ -312,6 +311,7 @@ def tile_stressed_factor_response_f2_kernel(
         nc.tensor.transpose(spec_ps[:], spec_rows[:], ident_b[:])
         nc.scalar.copy(out=spec_f[:], in_=spec_ps[:, 0:TILES])
         nc.scalar.activation(out=one[:], in_=one[:], func=ACT.Abs_reciprocal_sqrt)
+        EN = (nc.scalar, nc.scalar, nc.scalar, nc.vector, nc.scalar, nc.scalar, nc.scalar, nc.vector, nc.vector, nc.vector, nc.vector, nc.vector, nc.scalar, nc.scalar, nc.scalar, nc.scalar, nc.vector, nc.vector, nc.vector, nc.scalar)
         first, second = range(0, 4), range(4, 8)
         for j in first:
             y_mm(j)
@@ -332,10 +332,10 @@ def tile_stressed_factor_response_f2_kernel(
         quantise_z(1, 1)
         turn(0, 0)
         for j in first:
-            u_out(j, 0, nc.scalar)
+            u_out(j, 0, EN[j])
         turn(0, 1)
         for j in first:
-            u_out(j, 1, nc.scalar)
+            u_out(j, 1, EN[4 + j])
         for t in range(4):
             u_mm(1, 0, t)
             add_own(1, 0, t)
@@ -343,15 +343,15 @@ def tile_stressed_factor_response_f2_kernel(
             y_mm(j)
             y_square(j)
             if j % 2:
-                y_out(j - 1, nc.scalar)
-                y_out(j, nc.vector)
+                y_out(j - 1, EN[8+ j - 4 + 0 - 1])
+                y_out(j, EN[8+ j - 4 + 0])
         for t in range(4):
             u_mm(1, 1, t)
             add_own(1, 1, t)
             if t == 1:
                 turn(1, 0)
                 for j in second:
-                    u_out(j, 0, nc.scalar)
+                    u_out(j, 0, EN[8 + j])
         turn(1, 1)
         for j in second:
-            u_out(j, 1, nc.vector if j % 2 else nc.scalar)
+            u_out(j, 1, EN[12 + j])

@@ -10,6 +10,7 @@ F32 = mybir.dt.float32
 BF16 = mybir.dt.bfloat16
 I32 = mybir.dt.int32
 U32 = mybir.dt.uint32
+U16 = mybir.dt.uint16
 U8 = mybir.dt.uint8
 FP8X4 = mybir.dt.float8_e4m3fn_x4
 FP4X4 = mybir.dt.float4_e2m1fn_x4
@@ -17,15 +18,34 @@ ACT = mybir.ActivationFunctionType
 ALU = mybir.AluOpType
 
 P = 128
-KG = ASSETS // 512
-FG = FACTORS // 512
-NH = 512
-HALVES = PORTFOLIOS // NH
+PACK = 4
+K_GROUP = P * PACK
+ASSET_GROUPS = ASSETS // K_GROUP
+FACTOR_GROUPS = FACTORS // K_GROUP
+HALF = 512
 TILES = PORTFOLIOS // P
+TILES_PER_HALF = HALF // P
+CODE_BYTES = 2
+QUADRANTS = 4
+WARM_UP_MATMULS = 11
 
 
 def tile_stressed_factor_response_f2_kernel(
-    tc, h_words, h_scales, b_words, b_scales, bench, vol, c_words, c_scales, own, l_words, l_scales, spec, out_0, out_1
+    tc,
+    h_words,
+    h_scales,
+    b_words,
+    b_scales,
+    bench,
+    vol,
+    c_words,
+    c_scales,
+    own,
+    l_words,
+    l_scales,
+    spec,
+    out_0,
+    out_1,
 ):
     nc = tc.nc
     with ExitStack() as ctx:
@@ -34,324 +54,312 @@ def tile_stressed_factor_response_f2_kernel(
         psum = ctx.enter_context(tc.psum_pool(name="psum", bufs=8))
         ctx.enter_context(tc.manual_schedule())
 
-        bw_raw = keep.tile([P, KG, 2 * FACTORS], U8, name="bw_raw", align_bytes=64)
-        bs_raw = keep.tile([P, KG, FACTORS], U8, name="bs_raw", align_bytes=64)
-        bw = keep.tile([P, KG, 2 * FACTORS], U8, name="bw", align_bytes=64)
-        bs = keep.tile([P, KG, FACTORS], U8, name="bs", align_bytes=64)
-        hw = keep.tile([P, KG, 2 * PORTFOLIOS], U8, name="hw", align_bytes=64)
-        hs = keep.tile([P, KG, PORTFOLIOS], U8, name="hs", align_bytes=64)
-        cw_raw = keep.tile([P, FG, 2 * FACTORS], U8, name="cw_raw", align_bytes=64)
-        cs_raw = keep.tile([P, FG, FACTORS], U8, name="cs_raw", align_bytes=64)
-        cw = keep.tile([P, FG, 2 * FACTORS], U8, name="cw", align_bytes=64)
-        cs = keep.tile([P, FG, FACTORS], U8, name="cs", align_bytes=64)
-        lw = keep.tile([P, FG, 2 * DIRECTIONS], U8, name="lw", align_bytes=64)
-        ls = keep.tile([P, FG, DIRECTIONS], U8, name="ls", align_bytes=64)
-        bench_b = keep.tile([P, FG, 4], BF16, name="bench_b")
-        vol_b = keep.tile([P, FG, 4], BF16, name="vol_b")
-        own_b = keep.tile([P, FG, 4], BF16, name="own_b")
-        neg_bench = keep.tile([P, FG * 4], F32, name="neg_bench")
+        b_codes_raw = keep.tile([P, ASSET_GROUPS, CODE_BYTES * FACTORS], U8, name="b_codes_raw", align_bytes=64)
+        b_bytes_raw = keep.tile([P, ASSET_GROUPS, FACTORS], U8, name="b_bytes_raw", align_bytes=64)
+        b_codes = keep.tile([P, ASSET_GROUPS, CODE_BYTES * FACTORS], U8, name="b_codes", align_bytes=64)
+        b_bytes = keep.tile([P, ASSET_GROUPS, FACTORS], U8, name="b_bytes", align_bytes=64)
+        h_codes = keep.tile([P, ASSET_GROUPS, CODE_BYTES * PORTFOLIOS], U8, name="h_codes", align_bytes=64)
+        h_bytes = keep.tile([P, ASSET_GROUPS, PORTFOLIOS], U8, name="h_bytes", align_bytes=64)
+        c_codes_raw = keep.tile([P, FACTOR_GROUPS, CODE_BYTES * FACTORS], U8, name="c_codes_raw", align_bytes=64)
+        c_bytes_raw = keep.tile([P, FACTOR_GROUPS, FACTORS], U8, name="c_bytes_raw", align_bytes=64)
+        c_codes = keep.tile([P, FACTOR_GROUPS, CODE_BYTES * FACTORS], U8, name="c_codes", align_bytes=64)
+        c_bytes = keep.tile([P, FACTOR_GROUPS, FACTORS], U8, name="c_bytes", align_bytes=64)
+        l_codes = keep.tile([P, FACTOR_GROUPS, CODE_BYTES * DIRECTIONS], U8, name="l_codes", align_bytes=64)
+        l_bytes = keep.tile([P, FACTOR_GROUPS, DIRECTIONS], U8, name="l_bytes", align_bytes=64)
+
+        bench_b = keep.tile([P, FACTOR_GROUPS, PACK], BF16, name="bench_b")
+        vol_b = keep.tile([P, FACTOR_GROUPS, PACK], BF16, name="vol_b")
+        own_b = keep.tile([P, FACTOR_GROUPS, PACK], BF16, name="own_b")
+        minus_bench = keep.tile([P, FACTOR_GROUPS * PACK], F32, name="minus_bench")
+        vol_f = keep.tile([P, FACTOR_GROUPS * PACK], F32, name="vol_f")
+
         spec_rows = keep.tile([P, P], BF16, name="spec_rows")
         spec_f = keep.tile([P, TILES], F32, name="spec_f")
-        ident_b = keep.tile([P, P], BF16, name="ident_b")
-        ident = keep.tile([P, P], F32, name="ident")
+        mean_square = keep.tile([P, TILES], F32, name="mean_square")
+        inv_sigma = keep.tile([P, TILES], F32, name="inv_sigma")
+
+        identity_b = keep.tile([P, P], BF16, name="identity_b")
+        identity = keep.tile([P, P], F32, name="identity")
+        zero = keep.tile([P, 1], F32, name="zero")
         one = keep.tile([P, 1], F32, name="one")
-        ms = keep.tile([P, TILES], F32, name="ms")
-        rs = keep.tile([P, TILES], F32, name="rs")
-        warm = keep.tile([P, 1], F32, name="warm")
         idle = keep.tile([P, 512], BF16, name="idle")
 
-        def flat_i32(t):
-            return t[:].rearrange("p g n -> p (g n)").bitcast(I32)
+        def words(tile):
+            return tile[:].rearrange("p g n -> p (g n)").bitcast(I32)
 
-        def load_scales(plane, src):
-            for q in range(4):
+        nc.vector.memset(words(b_bytes_raw), 0)
+        nc.vector.memset(zero[:], 0.0)
+        nc.gpsimd.memset(idle[:], 0.0)
+        nc.gpsimd.memset(words(h_bytes), 0)
+        nc.gpsimd.memset(words(c_bytes_raw), 0)
+        nc.gpsimd.memset(spec_rows[:], 0.0)
+        nc.gpsimd.memset(words(l_bytes), 0)
+        nc.gpsimd.memset(one[:], 1.0)
+        make_identity(nc, identity[:])
+        make_identity(nc, identity_b[:])
+        nc.scalar.activation(out=zero[:], in_=zero[:], func=ACT.Tanh)
+
+        def load_scales(tile, src):
+            for q in range(QUADRANTS):
                 nc.sync.dma_start(
-                    out=plane[32 * q : 32 * q + 4, :, :].bitcast(I32),
+                    out=tile[32 * q : 32 * q + 4, :, :].bitcast(I32),
                     in_=src[:, 4 * q : 4 * q + 4, :].rearrange("g r n -> r g n").bitcast(I32),
                 )
 
-        def by_factor(v):
-            return v.rearrange("(g p t) -> p g t", g=FG, t=4)
+        def load_codes(tile, src):
+            nc.sync.dma_start(out=tile[:].bitcast(I32), in_=src.rearrange("g p n -> p g n").bitcast(I32))
 
-        nc.gpsimd.memset(idle[:], 0.0)
-        nc.vector.memset(flat_i32(hs), 0)
-        nc.gpsimd.memset(flat_i32(bs_raw), 0)
-        nc.vector.memset(warm[:], 0.0)
-        nc.gpsimd.memset(flat_i32(cs_raw), 0)
-        nc.gpsimd.memset(spec_rows[:], 0.0)
-        nc.gpsimd.memset(flat_i32(ls), 0)
-        nc.gpsimd.memset(one[:], 1.0)
-        make_identity(nc, ident[:])
-        make_identity(nc, ident_b[:])
+        def load_factor_vector(tile, src):
+            nc.sync.dma_start(out=tile[:], in_=src.rearrange("(f p t) -> p f t", f=FACTOR_GROUPS, t=PACK))
 
-        def load_b(g):
-            nc.sync.dma_start(out=bw_raw[:, g, :].bitcast(I32), in_=b_words[g].bitcast(I32))
+        first_half = slice(0, CODE_BYTES * HALF)
+        second_half = slice(CODE_BYTES * HALF, CODE_BYTES * PORTFOLIOS)
 
-        def load_h(g, h):
-            cols = slice(2 * NH * h, 2 * NH * (h + 1))
-            nc.sync.dma_start(out=hw[:, g, cols].bitcast(I32), in_=h_words[g][:, cols].bitcast(I32))
+        def load_stage_1_group(g):
+            nc.sync.dma_start(out=b_codes_raw[:, g, :].bitcast(I32), in_=b_words[g].bitcast(I32))
+            nc.sync.dma_start(out=h_codes[:, g, first_half].bitcast(I32), in_=h_words[g][:, first_half].bitcast(I32))
 
-        nc.scalar.activation(out=warm[:], in_=warm[:], func=ACT.Tanh)
-        load_b(0)
-        load_h(0, 0)
-        load_scales(hs, h_scales)
-        load_scales(bs_raw, b_scales)
-        for g in range(1, KG):
-            load_b(g)
-            load_h(g, 0)
-        nc.sync.dma_start(out=bench_b[:], in_=by_factor(bench))
-        nc.sync.dma_start(out=vol_b[:], in_=by_factor(vol))
-        nc.sync.dma_start(out=cw_raw[:].bitcast(I32), in_=c_words.rearrange("g p n -> p g n").bitcast(I32))
-        half_1 = slice(2 * NH, 4 * NH)
-        nc.sync.dma_start(
-            out=hw[:, :, half_1].bitcast(I32), in_=h_words[:, :, half_1].rearrange("g p n -> p g n").bitcast(I32)
-        )
-        load_scales(cs_raw, c_scales)
-        nc.sync.dma_start(out=own_b[:], in_=by_factor(own))
+        load_stage_1_group(0)
+        load_scales(b_bytes_raw, b_scales)
+        load_scales(h_bytes, h_scales)
+        for g in range(1, ASSET_GROUPS):
+            load_stage_1_group(g)
+        load_factor_vector(bench_b, bench)
+        load_factor_vector(vol_b, vol)
+        load_codes(c_codes_raw, c_words)
+        for g in range(ASSET_GROUPS):
+            nc.sync.dma_start(out=h_codes[:, g, second_half].bitcast(I32), in_=h_words[g][:, second_half].bitcast(I32))
+        load_scales(c_bytes_raw, c_scales)
+        load_factor_vector(own_b, own)
         nc.sync.dma_start(out=spec_rows[0:TILES, :], in_=spec.rearrange("(j p) -> j p", p=P))
-        nc.sync.dma_start(out=lw[:].bitcast(I32), in_=l_words.rearrange("g p n -> p g n").bitcast(I32))
-        load_scales(ls, l_scales)
+        load_codes(l_codes, l_words)
+        load_scales(l_bytes, l_scales)
 
         idle_ps = psum.tile([P, 512], F32, tag="bank", name="idle_ps")
-        for i in range(14):
+        for i in range(WARM_UP_MATMULS):
             nc.tensor.matmul(out=idle_ps[:], lhsT=idle[:, 0:P], rhs=idle[:], start=True, stop=True)
 
-        xt, zt, zc, zs = {}, {}, {}, {}
-        bank = {}
-
-        def order_b(g, half):
-            c0 = half * 512
+        def regroup(out, in_, first, last):
             nc.vector.tensor_copy(
-                out=bw[:, g, :].rearrange("p (t c b) -> p t c b", t=4, b=2)[:, :, half * P : (half + 1) * P, :],
-                in_=bw_raw[:, g, 2 * c0 : 2 * c0 + 1024].rearrange("p (c t b) -> p t c b", t=4, b=2),
+                out=out.rearrange("p (t c) -> p t c", t=PACK)[:, :, first:last],
+                in_=in_[:, PACK * first : PACK * last].rearrange("p (c t) -> p t c", t=PACK),
             )
 
-        def order_bs(g, half):
-            nc.vector.tensor_copy(
-                out=bs[:, g, :].rearrange("p (t c) -> p t c", t=4)[:, :, half * P : (half + 1) * P],
-                in_=bs_raw[:, g, half * 512 : (half + 1) * 512].rearrange("p (c t) -> p t c", t=4),
-            )
+        def regroup_b(g, f):
+            regroup(b_codes[:, g, :].bitcast(U16), b_codes_raw[:, g, :].bitcast(U16), P * f, P * (f + 1))
+            regroup(b_bytes[:, g, :], b_bytes_raw[:, g, :], P * f, P * (f + 1))
 
-        def order_c(g):
-            nc.vector.tensor_copy(
-                out=cw[:, g, :].rearrange("p (t c b) -> p t c b", t=4, b=2),
-                in_=cw_raw[:, g, :].rearrange("p (c t b) -> p t c b", t=4, b=2),
-            )
+        def regroup_c(g):
+            regroup(c_codes[:, g, :].bitcast(U16), c_codes_raw[:, g, :].bitcast(U16), 0, FACTORS // PACK)
+            regroup(c_bytes[:, g, :], c_bytes_raw[:, g, :], 0, FACTORS // PACK)
 
-        def order_cs(g):
-            nc.vector.tensor_copy(
-                out=cs[:, g, :].rearrange("p (t c) -> p t c", t=4),
-                in_=cs_raw[:, g, :].rearrange("p (c t) -> p t c", t=4),
-            )
+        def factor_columns(codes, scales, g, f, t):
+            c0 = (FACTORS // PACK) * t + P * f
+            return codes[:, g, CODE_BYTES * c0 : CODE_BYTES * (c0 + P)].bitcast(FP4X4), scales[:, g, c0 : c0 + P]
 
-        def e_pass(h, fg, t, g):
+        e_banks, x_tiles, z_scaled, z_tiles, z_codes, z_bytes = {}, {}, {}, {}, {}, {}
+
+        def exposure_pass(h, f, t, g):
             if g == 0:
-                e_ps = psum.tile([P, NH], F32, tag="bank", name="e_ps")
-                bank[h, fg, t] = e_ps
-            c0 = t * 256 + fg * P
+                e_ps = psum.tile([P, HALF], F32, tag="bank", name="e_ps")
+                e_banks[h, f, t] = e_ps
+            stationary, stationary_scale = factor_columns(b_codes, b_bytes, g, f, t)
             nc.tensor.matmul_mx(
-                out=bank[h, fg, t][:],
-                lhsT=bw[:, g, 2 * c0 : 2 * c0 + 2 * P].bitcast(FP4X4),
-                lhsT_scale=bs[:, g, c0 : c0 + P],
-                rhs=hw[:, g, 2 * NH * h : 2 * NH * (h + 1)].bitcast(FP4X4),
-                rhs_scale=hs[:, g, NH * h : NH * (h + 1)],
+                out=e_banks[h, f, t][:],
+                lhsT=stationary,
+                lhsT_scale=stationary_scale,
+                rhs=h_codes[:, g, CODE_BYTES * HALF * h : CODE_BYTES * HALF * (h + 1)].bitcast(FP4X4),
+                rhs_scale=h_bytes[:, g, HALF * h : HALF * (h + 1)],
                 start=(g == 0),
-                stop=(g == KG - 1),
+                stop=(g == ASSET_GROUPS - 1),
             )
 
-        def tanh_e(h, fg, t):
+        def winsorise(h, f, t):
             if t == 0:
-                x = keep.tile([P, 4, NH], F32, name="x%d%d" % (h, fg))
-                xt[h, fg] = x
-            c = fg * 4 + t
+                x = keep.tile([P, PACK, HALF], F32, name="x%d%d" % (h, f))
+                x_tiles[h, f] = x
+            column = PACK * f + t
             nc.scalar.activation(
-                out=xt[h, fg][:, t, :], in_=bank[h, fg, t][:], func=ACT.Tanh, bias=neg_bench[:, c : c + 1], scale=1.0
-            )
-
-        def make_z(h, fg):
-            z = keep.tile([P, NH, 4], BF16, name="z%d%d" % (h, fg), align_bytes=64)
-            zt[h, fg] = z
-            nc.vector.tensor_tensor(
-                out=z[:],
-                in0=xt[h, fg][:].rearrange("p t n -> p n t"),
-                in1=vol_b[:, fg : fg + 1, :].to_broadcast([P, NH, 4]),
-                op=ALU.mult,
-            )
-
-        def quantise_z(h, fg):
-            codes = keep.tile([P, NH], U32, name="zc%d%d" % (h, fg), align_bytes=64)
-            scales = keep.tile([P, NH], U8, name="zs%d%d" % (h, fg), align_bytes=64)
-            zc[h, fg], zs[h, fg] = codes, scales
-            nc.vector.quantize_mx(
-                out=codes[:].bitcast(FP8X4), scales=scales[:], in_=zt[h, fg][:].rearrange("p n t -> p (n t)")
-            )
-
-        ybank, tbank, ubank, vt, us = {}, {}, {}, {}, {}
-
-        def y_mm(j):
-            h, c0 = j // 4, P * (j % 4)
-            y_ps = psum.tile([P, DIRECTIONS], F32, tag="bank", name="y_ps")
-            ybank[j] = y_ps
-            for g in range(FG):
-                nc.tensor.matmul_mx(
-                    out=y_ps[:],
-                    lhsT=zc[h, g][:, c0 : c0 + P].bitcast(FP8X4),
-                    lhsT_scale=zs[h, g][:, c0 : c0 + P],
-                    rhs=lw[:, g, :].bitcast(FP4X4),
-                    rhs_scale=ls[:, g, :],
-                    start=(g == 0),
-                    stop=(g == FG - 1),
-                )
-
-        def inverse_risk(j):
-            nc.scalar.activation(
-                out=rs[:, j : j + 1],
-                in_=ms[:, j : j + 1],
-                func=ACT.Abs_reciprocal_sqrt,
-                bias=spec_f[:, j : j + 1],
+                out=x_tiles[h, f][:, t, :],
+                in_=e_banks[h, f, t][:],
+                func=ACT.Tanh,
+                bias=minus_bench[:, column : column + 1],
                 scale=1.0,
             )
 
-        def y_square(j):
-            sq = work.tile([P, DIRECTIONS], BF16, name="sq", bufs=2)
-            nc.scalar.activation(
-                out=sq[:], in_=ybank[j][:], func=ACT.Square, scale=DIRECTIONS**-0.5, accum_out=ms[:, j : j + 1]
-            )
-            if j % 2:
-                inverse_risk(j - 1)
-                inverse_risk(j)
+        def scale_on_scalar(h, f):
+            zs = keep.tile([P, PACK, HALF], BF16, name="zs%d%d" % (h, f))
+            z_scaled[h, f] = zs
+            for t in range(PACK):
+                column = PACK * f + t
+                nc.scalar.activation(
+                    out=zs[:, t, :], in_=x_tiles[h, f][:, t, :], func=ACT.Copy, scale=vol_f[:, column : column + 1]
+                )
 
-        def scaled(engine, out, in_, j):
-            if engine is nc.scalar:
-                nc.scalar.activation(out=out, in_=in_, func=ACT.Copy, scale=rs[:, j : j + 1])
+        def interleave_z(h, f):
+            z = keep.tile([P, HALF, PACK], BF16, name="z%d%d" % (h, f), align_bytes=64)
+            z_tiles[h, f] = z
+            if (h, f) in z_scaled:
+                nc.vector.tensor_copy(out=z[:], in_=z_scaled[h, f][:].rearrange("p t n -> p n t"))
             else:
-                nc.vector.tensor_scalar(out=out, in0=in_, scalar1=rs[:, j : j + 1], scalar2=None, op0=ALU.mult)
+                nc.vector.tensor_tensor(
+                    out=z[:],
+                    in0=x_tiles[h, f][:].rearrange("p t n -> p n t"),
+                    in1=vol_b[:, f : f + 1, :].to_broadcast([P, HALF, PACK]),
+                    op=ALU.mult,
+                )
 
-        def y_out(j, engine):
-            y_sb = work.tile([P, DIRECTIONS], F32, name="y_sb")
-            scaled(engine, y_sb[:], ybank[j][:], j)
-            nc.sync.dma_start(out=out_1[P * j : P * (j + 1), :], in_=y_sb[:])
+        def quantise_z(h, f):
+            codes = keep.tile([P, HALF], U32, name="z_codes%d%d" % (h, f), align_bytes=64)
+            scales = keep.tile([P, HALF], U8, name="z_bytes%d%d" % (h, f), align_bytes=64)
+            z_codes[h, f], z_bytes[h, f] = codes, scales
+            nc.vector.quantize_mx(
+                out=codes[:].bitcast(FP8X4), scales=scales[:], in_=z_tiles[h, f][:].rearrange("p n t -> p (n t)")
+            )
 
-        def u_mm(h, fg, t, n0=0, n1=NH):
-            u_ps = psum.tile([P, NH], F32, tag="bank", name="u_ps")
-            ubank[h, fg, t] = u_ps
-            c0 = t * 256 + fg * P
-            width = NH if n1 - n0 == NH else P
-            for n in range(n0, n1, width):
-                for g in range(FG):
+        y_banks, u_banks, v_tiles, turned_banks, u_out_tiles = {}, {}, {}, {}, {}
+
+        def scaled_copy(engine, out, in_, j):
+            if engine is nc.scalar:
+                nc.scalar.activation(out=out, in_=in_, func=ACT.Copy, scale=inv_sigma[:, j : j + 1])
+            else:
+                nc.vector.tensor_scalar(
+                    out=out, in0=in_, scalar1=inv_sigma[:, j : j + 1], scalar2=None, op0=ALU.mult
+                )
+
+        def loadings_and_risk(tile_pair, engine):
+            for j in tile_pair:
+                h, n0 = j // TILES_PER_HALF, P * (j % TILES_PER_HALF)
+                y_ps = psum.tile([P, DIRECTIONS], F32, tag="bank", name="y_ps")
+                y_banks[j] = y_ps
+                for g in range(FACTOR_GROUPS):
                     nc.tensor.matmul_mx(
-                        out=u_ps[:, n : n + width],
-                        lhsT=cw[:, g, 2 * c0 : 2 * c0 + 2 * P].bitcast(FP4X4),
-                        lhsT_scale=cs[:, g, c0 : c0 + P],
-                        rhs=zc[h, g][:, n : n + width].bitcast(FP8X4),
-                        rhs_scale=zs[h, g][:, n : n + width],
+                        out=y_ps[:],
+                        lhsT=z_codes[h, g][:, n0 : n0 + P].bitcast(FP8X4),
+                        lhsT_scale=z_bytes[h, g][:, n0 : n0 + P],
+                        rhs=l_codes[:, g, :].bitcast(FP4X4),
+                        rhs_scale=l_bytes[:, g, :],
                         start=(g == 0),
-                        stop=(g == FG - 1),
+                        stop=(g == FACTOR_GROUPS - 1),
                     )
+                squares = work.tile([P, DIRECTIONS], BF16, name="squares", bufs=2)
+                nc.scalar.activation(
+                    out=squares[:],
+                    in_=y_ps[:],
+                    func=ACT.Square,
+                    scale=DIRECTIONS**-0.5,
+                    accum_out=mean_square[:, j : j + 1],
+                )
+            for j in tile_pair:
+                nc.scalar.activation(
+                    out=inv_sigma[:, j : j + 1],
+                    in_=mean_square[:, j : j + 1],
+                    func=ACT.Abs_reciprocal_sqrt,
+                    bias=spec_f[:, j : j + 1],
+                    scale=1.0,
+                )
+            for j in tile_pair:
+                y_sb = work.tile([P, DIRECTIONS], F32, name="y_sb")
+                scaled_copy(engine, y_sb[:], y_banks[j][:], j)
+                nc.sync.dma_start(out=out_1[P * j : P * (j + 1), :], in_=y_sb[:])
 
-        def add_own(h, fg, t, n0=0, n1=NH):
-            if t == 0 and n0 == 0:
-                v = keep.tile([P, 4, NH], F32, name="v%d%d" % (h, fg))
-                vt[h, fg] = v
-            nc.vector.scalar_tensor_tensor(
-                out=vt[h, fg][:, t, n0:n1],
-                in0=xt[h, fg][:, t, n0:n1],
-                scalar=own_b[:, fg, t : t + 1],
-                in1=ubank[h, fg, t][:, n0:n1],
-                op0=ALU.mult,
-                op1=ALU.add,
-            )
+        def response(h, f, places):
+            for t in places:
+                u_ps = psum.tile([P, HALF], F32, tag="bank", name="u_ps")
+                u_banks[h, f, t] = u_ps
+                for g in range(FACTOR_GROUPS):
+                    stationary, stationary_scale = factor_columns(c_codes, c_bytes, g, f, t)
+                    nc.tensor.matmul_mx(
+                        out=u_ps[:],
+                        lhsT=stationary,
+                        lhsT_scale=stationary_scale,
+                        rhs=z_codes[h, g][:].bitcast(FP8X4),
+                        rhs_scale=z_bytes[h, g][:],
+                        start=(g == 0),
+                        stop=(g == FACTOR_GROUPS - 1),
+                    )
+                if t == 0:
+                    v = keep.tile([P, PACK, HALF], F32, name="v%d%d" % (h, f))
+                    v_tiles[h, f] = v
+                nc.vector.scalar_tensor_tensor(
+                    out=v_tiles[h, f][:, t, :],
+                    in0=x_tiles[h, f][:, t, :],
+                    scalar=own_b[:, f, t : t + 1],
+                    in1=u_ps[:],
+                    op0=ALU.mult,
+                    op1=ALU.add,
+                )
 
-        def turn(h, fg, i0=0, i1=4):
-            for i in range(i0, i1):
-                t_ps = psum.tile([P, 4, P], F32, tag="bank", name="t_ps")
-                tbank[4 * h + i, fg] = t_ps
-            for t in range(4):
-                for i in range(i0, i1):
-                    nc.tensor.transpose(tbank[4 * h + i, fg][:, t, :], vt[h, fg][:, t, P * i : P * (i + 1)], ident[:])
+        def turn_and_store(h, f, engines):
+            tiles = range(TILES_PER_HALF * h, TILES_PER_HALF * (h + 1))
+            for j in tiles:
+                t_ps = psum.tile([P, PACK, P], F32, tag="bank", name="t_ps")
+                turned_banks[j] = t_ps
+            for j in tiles:
+                n0 = P * (j % TILES_PER_HALF)
+                for t in range(PACK):
+                    nc.tensor.transpose(turned_banks[j][:, t, :], v_tiles[h, f][:, t, n0 : n0 + P], identity[:])
+            for j, engine in zip(tiles, engines):
+                if f == 0:
+                    u_sb = work.tile([P, FACTORS], F32, name="u_sb", bufs=8)
+                    u_out_tiles[j] = u_sb
+                columns = slice(K_GROUP * f, K_GROUP * (f + 1))
+                scaled_copy(
+                    engine,
+                    u_out_tiles[j][:, columns].rearrange("p (m t) -> p m t", t=PACK),
+                    turned_banks[j][:].rearrange("p t m -> p m t"),
+                    j,
+                )
+                nc.sync.dma_start(out=out_0[P * j : P * (j + 1), columns], in_=u_out_tiles[j][:, columns])
 
-        def u_out(j, fg, engine):
-            if fg == 0:
-                u_sb = work.tile([P, FACTORS], F32, name="u_sb", bufs=8)
-                us[j] = u_sb
-            cols = slice(512 * fg, 512 * (fg + 1))
-            scaled(
-                engine,
-                us[j][:, cols].rearrange("p (m t) -> p m t", t=4),
-                tbank[j, fg][:].rearrange("p t m -> p m t"),
-                j,
-            )
-            nc.sync.dma_start(out=out_0[P * j : P * (j + 1), cols], in_=us[j][:, cols])
+        nc.scalar.activation(
+            out=minus_bench[:], in_=bench_b[:].rearrange("p f t -> p (f t)"), func=ACT.Copy, scale=-1.0
+        )
+        nc.scalar.copy(out=vol_f[:], in_=vol_b[:].rearrange("p f t -> p (f t)"))
 
-        nc.scalar.activation(out=neg_bench[:], in_=bench_b[:].rearrange("p g t -> p (g t)"), func=ACT.Copy, scale=-1.0)
-        for g in range(KG):
-            for fg in range(FG):
-                order_b(g, fg)
-                order_bs(g, fg)
-                for t in range(4):
-                    e_pass(0, fg, t, g)
-        for g in range(FG):
-            order_c(g)
-            order_cs(g)
-        for fg in range(FG):
-            for t in range(4):
-                tanh_e(0, fg, t)
-        make_z(0, 0)
-        make_z(0, 1)
-        quantise_z(0, 0)
-        quantise_z(0, 1)
-        for fg in range(FG):
-            for t in range(4):
-                for g in range(KG):
-                    e_pass(1, fg, t, g)
-                tanh_e(1, fg, t)
-        make_z(1, 0)
+        for g in range(ASSET_GROUPS):
+            for f in range(FACTOR_GROUPS):
+                regroup_b(g, f)
+                for t in range(PACK):
+                    exposure_pass(0, f, t, g)
+        for g in range(FACTOR_GROUPS):
+            regroup_c(g)
+        for f in range(FACTOR_GROUPS):
+            for t in range(PACK):
+                winsorise(0, f, t)
+        for f in range(FACTOR_GROUPS):
+            interleave_z(0, f)
+        for f in range(FACTOR_GROUPS):
+            quantise_z(0, f)
+
+        for f in range(FACTOR_GROUPS):
+            for t in range(PACK):
+                for g in range(ASSET_GROUPS):
+                    exposure_pass(1, f, t, g)
+                winsorise(1, f, t)
+            if f == 0:
+                scale_on_scalar(1, 0)
+        interleave_z(1, 0)
 
         spec_ps = psum.tile([P, P], BF16, tag="bank", name="spec_ps")
-        nc.tensor.transpose(spec_ps[:], spec_rows[:], ident_b[:])
+        nc.tensor.transpose(spec_ps[:], spec_rows[:], identity_b[:])
         nc.scalar.copy(out=spec_f[:], in_=spec_ps[:, 0:TILES])
         nc.scalar.activation(out=one[:], in_=one[:], func=ACT.Abs_reciprocal_sqrt)
-        EN = (nc.scalar, nc.scalar, nc.scalar, nc.vector, nc.scalar, nc.scalar, nc.scalar, nc.vector, nc.vector, nc.vector, nc.vector, nc.vector, nc.scalar, nc.scalar, nc.scalar, nc.scalar, nc.vector, nc.vector, nc.vector, nc.scalar)
-        first, second = range(0, 4), range(4, 8)
-        for j in first:
-            y_mm(j)
-            y_square(j)
-            if j % 2:
-                y_out(j - 1, nc.scalar)
-                y_out(j, nc.scalar)
-            if j == 1:
-                for t in range(4):
-                    u_mm(0, 0, t)
-                make_z(1, 1)
-                for t in range(4):
-                    add_own(0, 0, t)
+
+        S, V = nc.scalar, nc.vector
+        loadings_and_risk((0, 1), S)
+        interleave_z(1, 1)
+        response(0, 0, range(PACK))
         quantise_z(1, 0)
-        for t in range(4):
-            u_mm(0, 1, t)
-            add_own(0, 1, t)
         quantise_z(1, 1)
-        turn(0, 0)
-        for j in first:
-            u_out(j, 0, EN[j])
-        turn(0, 1)
-        for j in first:
-            u_out(j, 1, EN[4 + j])
-        for t in range(4):
-            u_mm(1, 0, t)
-            add_own(1, 0, t)
-        for j in second:
-            y_mm(j)
-            y_square(j)
-            if j % 2:
-                y_out(j - 1, EN[8+ j - 4 + 0 - 1])
-                y_out(j, EN[8+ j - 4 + 0])
-        for t in range(4):
-            u_mm(1, 1, t)
-            add_own(1, 1, t)
-            if t == 1:
-                turn(1, 0)
-                for j in second:
-                    u_out(j, 0, EN[8 + j])
-        turn(1, 1)
-        for j in second:
-            u_out(j, 1, EN[12 + j])
+        loadings_and_risk((2, 3), S)
+        response(0, 1, range(PACK))
+        turn_and_store(0, 0, (S, S, S, V))
+        loadings_and_risk((4, 5), V)
+        loadings_and_risk((6, 7), V)
+        turn_and_store(0, 1, (S, S, S, V))
+        response(1, 0, range(PACK))
+        response(1, 1, (0, 1))
+        turn_and_store(1, 0, (S, S, S, S))
+        response(1, 1, (2, 3))
+        turn_and_store(1, 1, (V, V, V, S))

from contextlib import ExitStack

import concourse.mybir as mybir
from concourse.masks import make_identity

ASSETS, PORTFOLIOS, FACTORS, DIRECTIONS = 2048, 1024, 1024, 512
FLOPS = 2 * PORTFOLIOS * (ASSETS * FACTORS + FACTORS * FACTORS + FACTORS * DIRECTIONS)

F32 = mybir.dt.float32
BF16 = mybir.dt.bfloat16
I32 = mybir.dt.int32
U32 = mybir.dt.uint32
U16 = mybir.dt.uint16
U8 = mybir.dt.uint8
FP8X4 = mybir.dt.float8_e4m3fn_x4
FP4X4 = mybir.dt.float4_e2m1fn_x4
ACT = mybir.ActivationFunctionType
ALU = mybir.AluOpType

P = 128
PACK = 4
K_GROUP = P * PACK
ASSET_GROUPS = ASSETS // K_GROUP
FACTOR_GROUPS = FACTORS // K_GROUP
HALF = 512
TILES = PORTFOLIOS // P
TILES_PER_HALF = HALF // P
CODE_BYTES = 2
QUADRANTS = 4
WARM_UP_MATMULS = 11


def tile_stressed_factor_response_f2_kernel(
    tc,
    h_words,
    h_scales,
    b_words,
    b_scales,
    bench,
    vol,
    c_words,
    c_scales,
    own,
    l_words,
    l_scales,
    spec,
    out_0,
    out_1,
):
    nc = tc.nc
    with ExitStack() as ctx:
        keep = ctx.enter_context(tc.tile_pool(name="keep", bufs=1))
        work = ctx.enter_context(tc.tile_pool(name="work", bufs=4))
        psum = ctx.enter_context(tc.psum_pool(name="psum", bufs=8))
        ctx.enter_context(tc.manual_schedule())

        b_codes_raw = keep.tile([P, ASSET_GROUPS, CODE_BYTES * FACTORS], U8, name="b_codes_raw", align_bytes=64)
        b_bytes_raw = keep.tile([P, ASSET_GROUPS, FACTORS], U8, name="b_bytes_raw", align_bytes=64)
        b_codes = keep.tile([P, ASSET_GROUPS, CODE_BYTES * FACTORS], U8, name="b_codes", align_bytes=64)
        b_bytes = keep.tile([P, ASSET_GROUPS, FACTORS], U8, name="b_bytes", align_bytes=64)
        h_codes = keep.tile([P, ASSET_GROUPS, CODE_BYTES * PORTFOLIOS], U8, name="h_codes", align_bytes=64)
        h_bytes = keep.tile([P, ASSET_GROUPS, PORTFOLIOS], U8, name="h_bytes", align_bytes=64)
        c_codes_raw = keep.tile([P, FACTOR_GROUPS, CODE_BYTES * FACTORS], U8, name="c_codes_raw", align_bytes=64)
        c_bytes_raw = keep.tile([P, FACTOR_GROUPS, FACTORS], U8, name="c_bytes_raw", align_bytes=64)
        c_codes = keep.tile([P, FACTOR_GROUPS, CODE_BYTES * FACTORS], U8, name="c_codes", align_bytes=64)
        c_bytes = keep.tile([P, FACTOR_GROUPS, FACTORS], U8, name="c_bytes", align_bytes=64)
        l_codes = keep.tile([P, FACTOR_GROUPS, CODE_BYTES * DIRECTIONS], U8, name="l_codes", align_bytes=64)
        l_bytes = keep.tile([P, FACTOR_GROUPS, DIRECTIONS], U8, name="l_bytes", align_bytes=64)

        bench_b = keep.tile([P, FACTOR_GROUPS, PACK], BF16, name="bench_b")
        vol_b = keep.tile([P, FACTOR_GROUPS, PACK], BF16, name="vol_b")
        own_b = keep.tile([P, FACTOR_GROUPS, PACK], BF16, name="own_b")
        minus_bench = keep.tile([P, FACTOR_GROUPS * PACK], F32, name="minus_bench")
        vol_f = keep.tile([P, FACTOR_GROUPS * PACK], F32, name="vol_f")

        spec_rows = keep.tile([P, P], BF16, name="spec_rows")
        spec_f = keep.tile([P, TILES], F32, name="spec_f")
        mean_square = keep.tile([P, TILES], F32, name="mean_square")
        inv_sigma = keep.tile([P, TILES], F32, name="inv_sigma")

        identity_b = keep.tile([P, P], BF16, name="identity_b")
        identity = keep.tile([P, P], F32, name="identity")
        zero = keep.tile([P, 1], F32, name="zero")
        one = keep.tile([P, 1], F32, name="one")
        idle = keep.tile([P, 512], BF16, name="idle")

        def words(tile):
            return tile[:].rearrange("p g n -> p (g n)").bitcast(I32)

        nc.vector.memset(words(b_bytes_raw), 0)
        nc.vector.memset(zero[:], 0.0)
        nc.gpsimd.memset(idle[:], 0.0)
        nc.gpsimd.memset(words(h_bytes), 0)
        nc.gpsimd.memset(words(c_bytes_raw), 0)
        nc.gpsimd.memset(spec_rows[:], 0.0)
        nc.gpsimd.memset(words(l_bytes), 0)
        nc.gpsimd.memset(one[:], 1.0)
        make_identity(nc, identity[:])
        make_identity(nc, identity_b[:])
        nc.scalar.activation(out=zero[:], in_=zero[:], func=ACT.Tanh)

        def load_scales(tile, src):
            for q in range(QUADRANTS):
                nc.sync.dma_start(
                    out=tile[32 * q : 32 * q + 4, :, :].bitcast(I32),
                    in_=src[:, 4 * q : 4 * q + 4, :].rearrange("g r n -> r g n").bitcast(I32),
                )

        def load_codes(tile, src):
            nc.sync.dma_start(out=tile[:].bitcast(I32), in_=src.rearrange("g p n -> p g n").bitcast(I32))

        def load_factor_vector(tile, src):
            nc.sync.dma_start(out=tile[:], in_=src.rearrange("(f p t) -> p f t", f=FACTOR_GROUPS, t=PACK))

        first_half = slice(0, CODE_BYTES * HALF)
        second_half = slice(CODE_BYTES * HALF, CODE_BYTES * PORTFOLIOS)

        def load_stage_1_group(g):
            nc.sync.dma_start(out=b_codes_raw[:, g, :].bitcast(I32), in_=b_words[g].bitcast(I32))
            nc.sync.dma_start(out=h_codes[:, g, first_half].bitcast(I32), in_=h_words[g][:, first_half].bitcast(I32))

        load_stage_1_group(0)
        load_scales(b_bytes_raw, b_scales)
        load_scales(h_bytes, h_scales)
        for g in range(1, ASSET_GROUPS):
            load_stage_1_group(g)
        load_factor_vector(bench_b, bench)
        load_factor_vector(vol_b, vol)
        load_codes(c_codes_raw, c_words)
        for g in range(ASSET_GROUPS):
            nc.sync.dma_start(out=h_codes[:, g, second_half].bitcast(I32), in_=h_words[g][:, second_half].bitcast(I32))
        load_scales(c_bytes_raw, c_scales)
        load_factor_vector(own_b, own)
        nc.sync.dma_start(out=spec_rows[0:TILES, :], in_=spec.rearrange("(j p) -> j p", p=P))
        load_codes(l_codes, l_words)
        load_scales(l_bytes, l_scales)

        idle_ps = psum.tile([P, 512], F32, tag="bank", name="idle_ps")
        for i in range(WARM_UP_MATMULS):
            nc.tensor.matmul(out=idle_ps[:], lhsT=idle[:, 0:P], rhs=idle[:], start=True, stop=True)

        def regroup(out, in_, first, last):
            nc.vector.tensor_copy(
                out=out.rearrange("p (t c) -> p t c", t=PACK)[:, :, first:last],
                in_=in_[:, PACK * first : PACK * last].rearrange("p (c t) -> p t c", t=PACK),
            )

        def regroup_b(g, f):
            regroup(b_codes[:, g, :].bitcast(U16), b_codes_raw[:, g, :].bitcast(U16), P * f, P * (f + 1))
            regroup(b_bytes[:, g, :], b_bytes_raw[:, g, :], P * f, P * (f + 1))

        def regroup_c(g):
            regroup(c_codes[:, g, :].bitcast(U16), c_codes_raw[:, g, :].bitcast(U16), 0, FACTORS // PACK)
            regroup(c_bytes[:, g, :], c_bytes_raw[:, g, :], 0, FACTORS // PACK)

        def factor_columns(codes, scales, g, f, t):
            c0 = (FACTORS // PACK) * t + P * f
            return codes[:, g, CODE_BYTES * c0 : CODE_BYTES * (c0 + P)].bitcast(FP4X4), scales[:, g, c0 : c0 + P]

        e_banks, x_tiles, z_scaled, z_tiles, z_codes, z_bytes = {}, {}, {}, {}, {}, {}

        def exposure_pass(h, f, t, g):
            if g == 0:
                e_ps = psum.tile([P, HALF], F32, tag="bank", name="e_ps")
                e_banks[h, f, t] = e_ps
            stationary, stationary_scale = factor_columns(b_codes, b_bytes, g, f, t)
            nc.tensor.matmul_mx(
                out=e_banks[h, f, t][:],
                lhsT=stationary,
                lhsT_scale=stationary_scale,
                rhs=h_codes[:, g, CODE_BYTES * HALF * h : CODE_BYTES * HALF * (h + 1)].bitcast(FP4X4),
                rhs_scale=h_bytes[:, g, HALF * h : HALF * (h + 1)],
                start=(g == 0),
                stop=(g == ASSET_GROUPS - 1),
            )

        def winsorise(h, f, t):
            if t == 0:
                x = keep.tile([P, PACK, HALF], F32, name="x%d%d" % (h, f))
                x_tiles[h, f] = x
            column = PACK * f + t
            nc.scalar.activation(
                out=x_tiles[h, f][:, t, :],
                in_=e_banks[h, f, t][:],
                func=ACT.Tanh,
                bias=minus_bench[:, column : column + 1],
                scale=1.0,
            )

        def scale_on_scalar(h, f):
            zs = keep.tile([P, PACK, HALF], BF16, name="zs%d%d" % (h, f))
            z_scaled[h, f] = zs
            for t in range(PACK):
                column = PACK * f + t
                nc.scalar.activation(
                    out=zs[:, t, :], in_=x_tiles[h, f][:, t, :], func=ACT.Copy, scale=vol_f[:, column : column + 1]
                )

        def interleave_z(h, f):
            z = keep.tile([P, HALF, PACK], BF16, name="z%d%d" % (h, f), align_bytes=64)
            z_tiles[h, f] = z
            if (h, f) in z_scaled:
                nc.vector.tensor_copy(out=z[:], in_=z_scaled[h, f][:].rearrange("p t n -> p n t"))
            else:
                nc.vector.tensor_tensor(
                    out=z[:],
                    in0=x_tiles[h, f][:].rearrange("p t n -> p n t"),
                    in1=vol_b[:, f : f + 1, :].to_broadcast([P, HALF, PACK]),
                    op=ALU.mult,
                )

        def quantise_z(h, f):
            codes = keep.tile([P, HALF], U32, name="z_codes%d%d" % (h, f), align_bytes=64)
            scales = keep.tile([P, HALF], U8, name="z_bytes%d%d" % (h, f), align_bytes=64)
            z_codes[h, f], z_bytes[h, f] = codes, scales
            nc.vector.quantize_mx(
                out=codes[:].bitcast(FP8X4), scales=scales[:], in_=z_tiles[h, f][:].rearrange("p n t -> p (n t)")
            )

        y_banks, u_banks, v_tiles, turned_banks, u_out_tiles = {}, {}, {}, {}, {}

        def scaled_copy(engine, out, in_, j):
            if engine is nc.scalar:
                nc.scalar.activation(out=out, in_=in_, func=ACT.Copy, scale=inv_sigma[:, j : j + 1])
            else:
                nc.vector.tensor_scalar(
                    out=out, in0=in_, scalar1=inv_sigma[:, j : j + 1], scalar2=None, op0=ALU.mult
                )

        def loadings_and_risk(tile_pair, engine):
            for j in tile_pair:
                h, n0 = j // TILES_PER_HALF, P * (j % TILES_PER_HALF)
                y_ps = psum.tile([P, DIRECTIONS], F32, tag="bank", name="y_ps")
                y_banks[j] = y_ps
                for g in range(FACTOR_GROUPS):
                    nc.tensor.matmul_mx(
                        out=y_ps[:],
                        lhsT=z_codes[h, g][:, n0 : n0 + P].bitcast(FP8X4),
                        lhsT_scale=z_bytes[h, g][:, n0 : n0 + P],
                        rhs=l_codes[:, g, :].bitcast(FP4X4),
                        rhs_scale=l_bytes[:, g, :],
                        start=(g == 0),
                        stop=(g == FACTOR_GROUPS - 1),
                    )
                squares = work.tile([P, DIRECTIONS], BF16, name="squares", bufs=2)
                nc.scalar.activation(
                    out=squares[:],
                    in_=y_ps[:],
                    func=ACT.Square,
                    scale=DIRECTIONS**-0.5,
                    accum_out=mean_square[:, j : j + 1],
                )
            for j in tile_pair:
                nc.scalar.activation(
                    out=inv_sigma[:, j : j + 1],
                    in_=mean_square[:, j : j + 1],
                    func=ACT.Abs_reciprocal_sqrt,
                    bias=spec_f[:, j : j + 1],
                    scale=1.0,
                )
            for j in tile_pair:
                y_sb = work.tile([P, DIRECTIONS], F32, name="y_sb")
                scaled_copy(engine, y_sb[:], y_banks[j][:], j)
                nc.sync.dma_start(out=out_1[P * j : P * (j + 1), :], in_=y_sb[:])

        def response(h, f, places):
            for t in places:
                u_ps = psum.tile([P, HALF], F32, tag="bank", name="u_ps")
                u_banks[h, f, t] = u_ps
                for g in range(FACTOR_GROUPS):
                    stationary, stationary_scale = factor_columns(c_codes, c_bytes, g, f, t)
                    nc.tensor.matmul_mx(
                        out=u_ps[:],
                        lhsT=stationary,
                        lhsT_scale=stationary_scale,
                        rhs=z_codes[h, g][:].bitcast(FP8X4),
                        rhs_scale=z_bytes[h, g][:],
                        start=(g == 0),
                        stop=(g == FACTOR_GROUPS - 1),
                    )
                if t == 0:
                    v = keep.tile([P, PACK, HALF], F32, name="v%d%d" % (h, f))
                    v_tiles[h, f] = v
                nc.vector.scalar_tensor_tensor(
                    out=v_tiles[h, f][:, t, :],
                    in0=x_tiles[h, f][:, t, :],
                    scalar=own_b[:, f, t : t + 1],
                    in1=u_ps[:],
                    op0=ALU.mult,
                    op1=ALU.add,
                )

        def turn_and_store(h, f, engines):
            tiles = range(TILES_PER_HALF * h, TILES_PER_HALF * (h + 1))
            for j in tiles:
                t_ps = psum.tile([P, PACK, P], F32, tag="bank", name="t_ps")
                turned_banks[j] = t_ps
            for j in tiles:
                n0 = P * (j % TILES_PER_HALF)
                for t in range(PACK):
                    nc.tensor.transpose(turned_banks[j][:, t, :], v_tiles[h, f][:, t, n0 : n0 + P], identity[:])
            for j, engine in zip(tiles, engines):
                if f == 0:
                    u_sb = work.tile([P, FACTORS], F32, name="u_sb", bufs=8)
                    u_out_tiles[j] = u_sb
                columns = slice(K_GROUP * f, K_GROUP * (f + 1))
                scaled_copy(
                    engine,
                    u_out_tiles[j][:, columns].rearrange("p (m t) -> p m t", t=PACK),
                    turned_banks[j][:].rearrange("p t m -> p m t"),
                    j,
                )
                nc.sync.dma_start(out=out_0[P * j : P * (j + 1), columns], in_=u_out_tiles[j][:, columns])

        nc.scalar.activation(
            out=minus_bench[:], in_=bench_b[:].rearrange("p f t -> p (f t)"), func=ACT.Copy, scale=-1.0
        )
        nc.scalar.copy(out=vol_f[:], in_=vol_b[:].rearrange("p f t -> p (f t)"))

        for g in range(ASSET_GROUPS):
            for f in range(FACTOR_GROUPS):
                regroup_b(g, f)
                for t in range(PACK):
                    exposure_pass(0, f, t, g)
        for g in range(FACTOR_GROUPS):
            regroup_c(g)
        for f in range(FACTOR_GROUPS):
            for t in range(PACK):
                winsorise(0, f, t)
        for f in range(FACTOR_GROUPS):
            interleave_z(0, f)
        for f in range(FACTOR_GROUPS):
            quantise_z(0, f)

        for f in range(FACTOR_GROUPS):
            for t in range(PACK):
                for g in range(ASSET_GROUPS):
                    exposure_pass(1, f, t, g)
                winsorise(1, f, t)
            if f == 0:
                scale_on_scalar(1, 0)
        interleave_z(1, 0)

        spec_ps = psum.tile([P, P], BF16, tag="bank", name="spec_ps")
        nc.tensor.transpose(spec_ps[:], spec_rows[:], identity_b[:])
        nc.scalar.copy(out=spec_f[:], in_=spec_ps[:, 0:TILES])
        nc.scalar.activation(out=one[:], in_=one[:], func=ACT.Abs_reciprocal_sqrt)

        S, V = nc.scalar, nc.vector
        loadings_and_risk((0, 1), S)
        interleave_z(1, 1)
        response(0, 0, range(PACK))
        quantise_z(1, 0)
        quantise_z(1, 1)
        loadings_and_risk((2, 3), S)
        response(0, 1, range(PACK))
        turn_and_store(0, 0, (S, S, S, V))
        loadings_and_risk((4, 5), V)
        loadings_and_risk((6, 7), V)
        turn_and_store(0, 1, (S, S, S, V))
        response(1, 0, range(PACK))
        response(1, 1, (0, 1))
        turn_and_store(1, 0, (S, S, S, S))
        response(1, 1, (2, 3))
        turn_and_store(1, 1, (V, V, V, S))
